import numpy as np
import ml_dtypes


def mxq(x, axis, fmt="e4m3"):
    dtype, down = {"e4m3": (ml_dtypes.float8_e4m3fn, 7), "e5m2": (ml_dtypes.float8_e5m2, 14)}[fmt]
    v = np.moveaxis(np.asarray(x, np.float32).astype(ml_dtypes.bfloat16).astype(np.float64), axis, -1)
    blocks = v.reshape(v.shape[:-1] + (-1, 32))
    amax = np.abs(blocks).max(-1, keepdims=True)
    byte = np.maximum(np.where(amax > 0, np.frexp(amax)[1] - 1 + 127, 0) - down, 1)
    scale = np.exp2(byte - 127.0)
    codes = (blocks / scale).astype(np.float32).astype(dtype).astype(np.float64)
    return np.moveaxis((codes * scale).reshape(v.shape), -1, axis)


WIDE = False


def mx_kscale(k):
    if not WIDE:
        return np.ones(k)
    levels = np.array([10, -10, 5, -5, 0])
    if k % 512:
        return np.exp2(np.random.permutation(np.resize(levels, k // 32))).repeat(32)
    a = np.empty((k // 512, 16))
    for p in range(k // 512):
        a[p, :8] = np.random.permutation(np.resize(levels, 8))
        for g in range(8):
            far = levels[np.abs(levels - a[p, g]) >= 10]
            a[p, g + 8] = far[np.random.randint(len(far))]
    return np.exp2(a.ravel()).repeat(32)


def f64(x):
    return np.asarray(x).astype(np.float64)


def striped(idx):
    return np.tile(idx.reshape(-1, 16).T, (8, 1)).astype(np.uint16)


def unstriped(offs):
    return offs[:16].T.reshape(-1).astype(np.int64)


E2M1 = np.array([0.0, 0.5, 1.0, 1.5, 2.0, 3.0, 4.0, 6.0, -0.0, -0.5, -1.0, -1.5, -2.0, -3.0, -4.0, -6.0])


def pack_fp4(w):
    k, n = w.shape
    w = f64(np.asarray(w, np.float32).astype(ml_dtypes.bfloat16)).reshape(k // 32, 32, n)
    amax = np.abs(w).max(1)
    mant, ex = np.frexp(amax / 6.0)
    byte = np.clip(np.where(amax > 0, np.where(mant > 0.5, ex, ex - 1) + 127, 1), 1, 254)
    scaled = (w * np.exp2(127.0 - byte)[:, None, :]).reshape(k, n).astype(np.float32)
    c = np.ascontiguousarray(scaled.reshape(k // 512, 128, 4, n).transpose(0, 1, 3, 2)).astype(ml_dtypes.float4_e2m1fn).view(np.uint8) & 0xF
    words = (c[..., 0::2] | (c[..., 1::2] << 4)).reshape(k // 512, 128, 2 * n)
    return np.ascontiguousarray(words), np.ascontiguousarray(byte.astype(np.uint8).reshape(k // 512, 16, n))


def unpack_fp4(words, scales):
    g, _, n = scales.shape
    words = np.ascontiguousarray(words).reshape(g, 128, n, 2)
    nib = np.empty((g, 128, n, 4), np.uint8)
    nib[..., 0::2] = words & 0xF
    nib[..., 1::2] = words >> 4
    vals = E2M1[nib] * np.repeat(np.exp2(scales.astype(np.float64) - 127.0), 8, axis=1)[..., None]
    return vals.transpose(0, 1, 3, 2).reshape(g * 512, n)


def silu(v):
    return v / (1.0 + np.exp(-np.maximum(v, -700.0)))


K, T, S, V, H, N, J, U = 512, 2048, 512, 256, 512, 256, 512, 512


def setup_inputs():
    n = np.random.standard_normal
    s = mx_kscale(K)[:, None]
    u = mx_kscale(H)
    r = mx_kscale(J)[:, None]
    packed_w2 = pack_fp4(n((H, N)) / np.sqrt(2 * H) / u[:, None])
    return {
        "xT": (n((K, T)) * s).astype(np.float32),
        "aT": (n((J, U)) * r).astype(np.float32),
        "w1": (n((K, H)) / np.sqrt(K) / s * u).astype(np.float32),
        "w3": (n((J, H)) / np.sqrt(J) / r).astype(np.float32),
        "w2_words": packed_w2[0],
        "w2_scales": packed_w2[1],
        "offs": striped(np.random.permutation(T)[:S]),
        "pos1": striped(np.random.permutation(S)[:V]),
        "pos2": striped(np.random.permutation(S)[:V]),
    }


def reference(xT, aT, w1, w3, w2_words, w2_scales, offs, pos1, pos2):
    xq = mxq(f64(xT)[:, unstriped(offs)], 0, "e4m3")
    h = silu(mxq(f64(w1), 0, "e4m3").T @ xq)
    f = mxq(f64(w3), 0, "e4m3").T @ mxq(f64(aT), 0, "e4m3")
    z = h[:, unstriped(pos1)] * f[:, :V] + h[:, unstriped(pos2)] * f[:, V:2 * V]
    return unpack_fp4(w2_words, w2_scales).T @ mxq(z, 0, "e4m3")

@@ -1,0 +1,181 @@
+from contextlib import ExitStack
+
+import concourse.mybir as mybir
+
+K, T, S, V, H, N = 512, 2048, 512, 256, 512, 256
+D = 2
+FLOPS = 2 * K * H * S + 2 * K * H * D * V + 2 * H * N * V
+
+F32 = mybir.dt.float32
+BF16 = mybir.dt.bfloat16
+I32 = mybir.dt.int32
+U32 = mybir.dt.uint32
+U16 = mybir.dt.uint16
+U8 = mybir.dt.uint8
+FP8X4 = mybir.dt.float8_e4m3fn_x4
+FP4X4 = mybir.dt.float4_e2m1fn_x4
+SILU = mybir.ActivationFunctionType.Silu
+MULT = mybir.AluOpType.mult
+ADD = mybir.AluOpType.add
+
+P = 128
+PACK = 4
+HALF = S // 2
+W3_VECTOR_M = 64
+
+
+def deal_weights(copy, grouped, raw, m0, m1):
+    copy(
+        out=grouped[:].rearrange("p t m j -> p m j t")[:, m0:m1],
+        in_=raw[:].rearrange("p j (m t) -> p m j t", t=PACK)[:, m0:m1],
+    )
+
+
+def quantize(nc, codes, scales, grouped):
+    nc.vector.quantize_mx(out=codes.bitcast(FP8X4), scales=scales, in_=grouped)
+
+
+def tile_picked_dime_none_e_kernel(tc, xT, aT, w1, w3, w2_words, w2_scales, offs, pos1, pos2, out):
+    nc = tc.nc
+    with ExitStack() as ctx:
+        keep = ctx.enter_context(tc.tile_pool(name="keep", bufs=1))
+        psum = ctx.enter_context(tc.psum_pool(name="psum", bufs=1))
+
+        def sb(shape, dtype, name):
+            return keep.tile(shape, dtype, name=name, align_bytes=64)
+
+        offs_sb = sb([P, S // 16], U16, "offs_sb")
+        pos_sb = [sb([P, V // 16], U16, "pos%d_sb" % d) for d in range(D)]
+        w1_raw = sb([P, PACK, H], F32, "w1_raw")
+        w3_raw = sb([P, PACK, H], F32, "w3_raw")
+        x_raw = [sb([P, T], F32, "x_raw%d" % j) for j in range(PACK)]
+        a_raw = [sb([P, PACK, V], F32, "a_raw%d" % d) for d in range(D)]
+        w2_codes = sb([P, 2 * N], U8, "w2_codes")
+        w2_plane = sb([P, N], U8, "w2_plane")
+        warm = sb([P, 2], F32, "warm")
+
+        nc.gpsimd.memset(warm[:, 0:1], 0.0)
+        nc.gpsimd.memset(w2_plane[:].bitcast(I32), 0)
+        nc.scalar.activation(out=warm[:, 1:2], in_=warm[:, 0:1], func=SILU)
+
+        x_rows = xT.rearrange("(p j) t -> p j t", j=PACK)
+        a_rows = aT.rearrange("(p j) u -> p j u", j=PACK)
+        nc.sync.dma_start(offs_sb[:], offs)
+        nc.sync.dma_start(out=w1_raw[:], in_=w1.rearrange("(p j) c -> p j c", j=PACK))
+        for j in range(PACK):
+            nc.sync.dma_start(out=x_raw[j][:], in_=x_rows[:, j, :])
+        nc.sync.dma_start(pos_sb[0][:], pos1)
+        nc.sync.dma_start(pos_sb[1][:], pos2)
+        nc.sync.dma_start(out=w3_raw[:], in_=w3.rearrange("(p j) c -> p j c", j=PACK))
+        for d in range(D):
+            nc.sync.dma_start(out=a_raw[d][:], in_=a_rows[:, :, d * V:(d + 1) * V])
+        nc.sync.dma_start(out=w2_codes[:].bitcast(I32), in_=w2_words[0].bitcast(I32))
+        for q in range(4):
+            nc.sync.dma_start(out=w2_plane[32 * q:32 * q + 4, :].bitcast(I32), in_=w2_scales[0, 4 * q:4 * q + 4, :].bitcast(I32))
+
+        w1_grouped = sb([P, PACK, P, PACK], BF16, "w1_grouped")
+        w1_codes = sb([P, H], U32, "w1_codes")
+        w1_plane = sb([P, H], U8, "w1_plane")
+        deal_weights(nc.scalar.copy, w1_grouped, w1_raw, 0, P)
+        quantize(nc, w1_codes[:], w1_plane[:], w1_grouped[:].rearrange("p t m j -> p (t m j)"))
+
+        x_grouped = sb([P, S, PACK], BF16, "x_grouped")
+        x_codes = sb([P, S], U32, "x_codes")
+        x_plane = sb([P, S], U8, "x_plane")
+        for j in range(PACK - 1):
+            nc.vector.tensor_copy(x_grouped[:, :, j], x_raw[j][:].indirect(offs_sb[:]))
+        h = [sb([P, S], F32, "h%d" % t) for t in range(PACK)]
+        for u in range(2):
+            cols = slice(u * HALF, (u + 1) * HALF)
+            nc.vector.tensor_copy(
+                x_grouped[:, cols, PACK - 1],
+                x_raw[PACK - 1][:].indirect(offs_sb[:, u * HALF // 16:(u + 1) * HALF // 16]),
+            )
+            quantize(nc, x_codes[:, cols], x_plane[:, cols], x_grouped[:, cols, :].rearrange("p s j -> p (s j)"))
+            for pair in range(2):
+                bank = psum.tile([P, 2, HALF], F32, name="h_bank%d%d" % (u, pair), tag="bank%d" % (2 * u + pair))
+                for e in range(2):
+                    t = 2 * pair + e
+                    nc.tensor.matmul_mx(
+                        out=bank[:, e, :],
+                        lhsT=w1_codes[:, t * P:(t + 1) * P].bitcast(FP8X4),
+                        lhsT_scale=w1_plane[:, t * P:(t + 1) * P],
+                        rhs=x_codes[:, cols].bitcast(FP8X4),
+                        rhs_scale=x_plane[:, cols],
+                        start=True,
+                        stop=True,
+                    )
+                for e in range(2):
+                    nc.scalar.activation(out=h[2 * pair + e][:, cols], in_=bank[:, e, :], func=SILU)
+
+        w3_grouped = sb([P, PACK, P, PACK], BF16, "w3_grouped")
+        w3_codes = sb([P, H], U32, "w3_codes")
+        w3_plane = sb([P, H], U8, "w3_plane")
+        deal_weights(nc.vector.tensor_copy, w3_grouped, w3_raw, 0, W3_VECTOR_M)
+        deal_weights(nc.scalar.copy, w3_grouped, w3_raw, W3_VECTOR_M, P)
+        quantize(nc, w3_codes[:], w3_plane[:], w3_grouped[:].rearrange("p t m j -> p (t m j)"))
+
+        f_banks = []
+        for d in range(D):
+            a_grouped = sb([P, V, PACK], BF16, "a_grouped%d" % d)
+            a_codes = sb([P, V], U32, "a_codes%d" % d)
+            a_plane = sb([P, V], U8, "a_plane%d" % d)
+            nc.scalar.copy(
+                out=a_grouped[:].rearrange("p (c i) j -> p c j i", i=4),
+                in_=a_raw[d][:].rearrange("p j (c i) -> p c j i", i=4),
+            )
+            quantize(nc, a_codes[:], a_plane[:], a_grouped[:].rearrange("p v j -> p (v j)"))
+            for pair in range(2):
+                bank = psum.tile([P, 2, V], F32, name="f_bank%d%d" % (d, pair), tag="bank%d" % (4 + 2 * d + pair))
+                for e in range(2):
+                    t = 2 * pair + e
+                    nc.tensor.matmul_mx(
+                        out=bank[:, e, :],
+                        lhsT=w3_codes[:, t * P:(t + 1) * P].bitcast(FP8X4),
+                        lhsT_scale=w3_plane[:, t * P:(t + 1) * P],
+                        rhs=a_codes[:].bitcast(FP8X4),
+                        rhs_scale=a_plane[:],
+                        start=True,
+                        stop=True,
+                    )
+                f_banks.append(bank)
+
+        picked = [sb([P, PACK, V], F32, "picked%d" % d) for d in range(D)]
+        for t in range(PACK):
+            for d in range(D):
+                nc.vector.tensor_copy(picked[d][:, t, :], h[t][:].indirect(pos_sb[d][:]))
+        term = [sb([P, PACK, V], F32, "term%d" % d) for d in range(D)]
+        for d in range(D):
+            for pair in range(2):
+                rows = slice(2 * pair, 2 * pair + 2)
+                nc.vector.tensor_tensor(term[d][:, rows, :], f_banks[2 * d + pair][:], picked[d][:, rows, :], MULT)
+
+        z_grouped = sb([P, V, PACK], BF16, "z_grouped")
+        z_codes = sb([P, V], U32, "z_codes")
+        z_plane = sb([P, V], U8, "z_plane")
+        nc.vector.tensor_tensor(
+            z_grouped[:].rearrange("p (c i) t -> p c t i", i=4),
+            term[0][:].rearrange("p t (c i) -> p c t i", i=4),
+            term[1][:].rearrange("p t (c i) -> p c t i", i=4),
+            ADD,
+        )
+        quantize(nc, z_codes[:], z_plane[:], z_grouped[:].rearrange("p v t -> p (v t)"))
+
+        for b in range(N // P):
+            bank = psum.tile([P, V], F32, name="out_bank%d" % b, tag="bank%d" % b)
+            nc.tensor.matmul_mx(
+                out=bank[:],
+                lhsT=w2_codes[:, 2 * b * P:2 * (b + 1) * P].bitcast(FP4X4),
+                lhsT_scale=w2_plane[:, b * P:(b + 1) * P],
+                rhs=z_codes[:].bitcast(FP8X4),
+                rhs_scale=z_plane[:],
+                start=True,
+                stop=True,
+            )
+            result = sb([P, V], F32, "result%d" % b)
+            if b == 0:
+                nc.scalar.copy(out=result[:], in_=bank[:])
+                nc.scalar.dma_start(out=out[b * P:(b + 1) * P, :], in_=result[:])
+            else:
+                nc.vector.tensor_copy(out=result[:], in_=bank[:])
+                nc.sync.dma_start(out=out[b * P:(b + 1) * P, :], in_=result[:])

@@ -21,13 +21,20 @@ ADD = mybir.AluOpType.add
 P = 128
 PACK = 4
 HALF = S // 2
-W3_VECTOR_M = 64
+W1_SCALAR_M = 80
 
 
 def deal_weights(copy, grouped, raw, m0, m1):
     copy(
         out=grouped[:].rearrange("p t m j -> p m j t")[:, m0:m1],
-        in_=raw[:].rearrange("p j (m t) -> p m j t", t=PACK)[:, m0:m1],
+        in_=raw[:].rearrange("p j (m t) -> p m j t", t=PACK),
+    )
+
+
+def interleave(copy, grouped, raw):
+    copy(
+        out=grouped[:].rearrange("p (c i) j -> p c j i", i=4),
+        in_=raw[:].rearrange("p j (c i) -> p c j i", i=4),
     )
 
 
@@ -41,12 +48,14 @@ def tile_picked_dime_none_e_kernel(tc, xT, aT, w1, w3, w2_words, w2_scales, offs
         keep = ctx.enter_context(tc.tile_pool(name="keep", bufs=1))
         psum = ctx.enter_context(tc.psum_pool(name="psum", bufs=1))
 
-        def sb(shape, dtype, name):
-            return keep.tile(shape, dtype, name=name, align_bytes=64)
+        def sb(shape, dtype, name, tag=None):
+            return keep.tile(shape, dtype, name=name, tag=tag or name, align_bytes=64)
 
         offs_sb = sb([P, S // 16], U16, "offs_sb")
         pos_sb = [sb([P, V // 16], U16, "pos%d_sb" % d) for d in range(D)]
-        w1_raw = sb([P, PACK, H], F32, "w1_raw")
+        w1_cut = PACK * W1_SCALAR_M
+        w1_raw_a = sb([P, PACK, w1_cut], F32, "w1_raw_a")
+        w1_raw_b = sb([P, PACK, H - w1_cut], F32, "w1_raw_b")
         w3_raw = sb([P, PACK, H], F32, "w3_raw")
         x_raw = [sb([P, T], F32, "x_raw%d" % j) for j in range(PACK)]
         a_raw = [sb([P, PACK, V], F32, "a_raw%d" % d) for d in range(D)]
@@ -54,128 +63,145 @@ def tile_picked_dime_none_e_kernel(tc, xT, aT, w1, w3, w2_words, w2_scales, offs
         w2_plane = sb([P, N], U8, "w2_plane")
         warm = sb([P, 2], F32, "warm")
 
-        nc.gpsimd.memset(warm[:, 0:1], 0.0)
-        nc.gpsimd.memset(w2_plane[:].bitcast(I32), 0)
+        nc.vector.memset(warm[:, 0:1], 0.0)
+        nc.vector.memset(w2_plane[:].bitcast(I32), 0)
         nc.scalar.activation(out=warm[:, 1:2], in_=warm[:, 0:1], func=SILU)
 
         x_rows = xT.rearrange("(p j) t -> p j t", j=PACK)
         a_rows = aT.rearrange("(p j) u -> p j u", j=PACK)
+        w1_rows = w1.rearrange("(p j) c -> p j c", j=PACK)
+        nc.sync.dma_start(out=x_raw[0][:], in_=x_rows[:, 0, :])
         nc.sync.dma_start(offs_sb[:], offs)
-        nc.sync.dma_start(out=w1_raw[:], in_=w1.rearrange("(p j) c -> p j c", j=PACK))
-        for j in range(PACK):
-            nc.sync.dma_start(out=x_raw[j][:], in_=x_rows[:, j, :])
+        nc.sync.dma_start(out=x_raw[1][:], in_=x_rows[:, 1, :])
         nc.sync.dma_start(pos_sb[0][:], pos1)
         nc.sync.dma_start(pos_sb[1][:], pos2)
+        nc.sync.dma_start(out=x_raw[2][:], in_=x_rows[:, 2, :])
+        nc.sync.dma_start(out=x_raw[3][:], in_=x_rows[:, 3, :])
+        nc.sync.dma_start(out=w1_raw_a[:], in_=w1_rows[:, :, :w1_cut])
+        nc.sync.dma_start(out=w1_raw_b[:], in_=w1_rows[:, :, w1_cut:])
+        nc.sync.dma_start(out=a_raw[0][:], in_=a_rows[:, :, :V])
         nc.sync.dma_start(out=w3_raw[:], in_=w3.rearrange("(p j) c -> p j c", j=PACK))
-        for d in range(D):
-            nc.sync.dma_start(out=a_raw[d][:], in_=a_rows[:, :, d * V:(d + 1) * V])
+        nc.sync.dma_start(out=a_raw[1][:], in_=a_rows[:, :, V:])
         nc.sync.dma_start(out=w2_codes[:].bitcast(I32), in_=w2_words[0].bitcast(I32))
         for q in range(4):
             nc.sync.dma_start(out=w2_plane[32 * q:32 * q + 4, :].bitcast(I32), in_=w2_scales[0, 4 * q:4 * q + 4, :].bitcast(I32))
 
+        x_grouped = sb([P, S, PACK], BF16, "x_grouped")
+        for j in range(PACK):
+            nc.vector.tensor_copy(x_grouped[:, :, j], x_raw[j][:].indirect(offs_sb[:]))
+        x_plane = [sb([P, HALF], U8, "x_plane%d" % u) for u in range(2)]
+        x_codes = [sb([P, HALF], U32, "x_codes0")]
+        quantize(nc, x_codes[0][:], x_plane[0][:], x_grouped[:, :HALF, :].rearrange("p s j -> p (s j)"))
+
         w1_grouped = sb([P, PACK, P, PACK], BF16, "w1_grouped")
         w1_codes = sb([P, H], U32, "w1_codes")
         w1_plane = sb([P, H], U8, "w1_plane")
-        deal_weights(nc.scalar.copy, w1_grouped, w1_raw, 0, P)
-        quantize(nc, w1_codes[:], w1_plane[:], w1_grouped[:].rearrange("p t m j -> p (t m j)"))
+        deal_weights(nc.scalar.copy, w1_grouped, w1_raw_a, 0, W1_SCALAR_M)
+        deal_weights(nc.vector.tensor_copy, w1_grouped, w1_raw_b, W1_SCALAR_M, P)
+        x_codes.append(sb([P, HALF], U32, "x_codes1", tag="w1_raw_b"))
+        quantize(nc, x_codes[1][:], x_plane[1][:], x_grouped[:, HALF:, :].rearrange("p s j -> p (s j)"))
 
-        x_grouped = sb([P, S, PACK], BF16, "x_grouped")
-        x_codes = sb([P, S], U32, "x_codes")
-        x_plane = sb([P, S], U8, "x_plane")
-        for j in range(PACK - 1):
-            nc.vector.tensor_copy(x_grouped[:, :, j], x_raw[j][:].indirect(offs_sb[:]))
-        h = [sb([P, S], F32, "h%d" % t) for t in range(PACK)]
-        for u in range(2):
-            cols = slice(u * HALF, (u + 1) * HALF)
-            nc.vector.tensor_copy(
-                x_grouped[:, cols, PACK - 1],
-                x_raw[PACK - 1][:].indirect(offs_sb[:, u * HALF // 16:(u + 1) * HALF // 16]),
+        def mx(bank, codes, plane, t, rhs_codes, rhs_plane, cols=slice(None)):
+            nc.tensor.matmul_mx(
+                out=bank,
+                lhsT=codes[:, t * P:(t + 1) * P].bitcast(FP8X4),
+                lhsT_scale=plane[:, t * P:(t + 1) * P],
+                rhs=rhs_codes[:, cols].bitcast(FP8X4),
+                rhs_scale=rhs_plane[:, cols],
+                start=True,
+                stop=True,
             )
-            quantize(nc, x_codes[:, cols], x_plane[:, cols], x_grouped[:, cols, :].rearrange("p s j -> p (s j)"))
-            for pair in range(2):
-                bank = psum.tile([P, 2, HALF], F32, name="h_bank%d%d" % (u, pair), tag="bank%d" % (2 * u + pair))
-                for e in range(2):
-                    t = 2 * pair + e
-                    nc.tensor.matmul_mx(
-                        out=bank[:, e, :],
-                        lhsT=w1_codes[:, t * P:(t + 1) * P].bitcast(FP8X4),
-                        lhsT_scale=w1_plane[:, t * P:(t + 1) * P],
-                        rhs=x_codes[:, cols].bitcast(FP8X4),
-                        rhs_scale=x_plane[:, cols],
-                        start=True,
-                        stop=True,
-                    )
-                for e in range(2):
-                    nc.scalar.activation(out=h[2 * pair + e][:, cols], in_=bank[:, e, :], func=SILU)
 
-        w3_grouped = sb([P, PACK, P, PACK], BF16, "w3_grouped")
+        h = [sb([P, S], F32, "h%d" % t) for t in range(PACK)]
+        for t in range(PACK):
+            cols = slice(t * P, (t + 1) * P)
+            quantize(nc, w1_codes[:, cols], w1_plane[:, cols], w1_grouped[:, t].rearrange("p m j -> p (m j)"))
+        for t in range(PACK):
+            if t == 0:
+                for u in range(2):
+                    bank = psum.tile([P, HALF], F32, name="h_bank0%d" % u, tag="bank%d" % u)
+                    mx(bank[:], w1_codes, w1_plane, t, x_codes[u], x_plane[u])
+                    nc.scalar.activation(out=h[t][:, u * HALF:(u + 1) * HALF], in_=bank[:], func=SILU)
+            else:
+                bank = psum.tile([P, S], F32, name="h_bank%d" % t, tag="bank%d" % (t + 1))
+                for u in range(2):
+                    mx(bank[:, u * HALF:(u + 1) * HALF], w1_codes, w1_plane, t, x_codes[u], x_plane[u])
+                nc.scalar.activation(out=h[t][:], in_=bank[:], func=SILU)
+
+        a_codes = []
+        a_plane = [sb([P, V], U8, "a_plane%d" % d) for d in range(D)]
+        a_grouped0 = sb([P, V, PACK], BF16, "a_grouped0", tag="x_grouped")
+        interleave(nc.vector.tensor_copy, a_grouped0, a_raw[0])
+
+        picked = {}
+
+        def pick(t, d):
+            nc.vector.tensor_copy(picked[d, t // 2][:, t % 2, :], h[t][:].indirect(pos_sb[d][:]))
+
+        for key in ((0, 0), (1, 0), (0, 1)):
+            picked[key] = sb([P, 2, V], F32, "picked%d%d" % key)
+        pick(0, 0)
+        pick(0, 1)
+        a_codes.append(sb([P, V], U32, "a_codes0", tag="h0"))
+        quantize(nc, a_codes[0][:], a_plane[0][:], a_grouped0[:].rearrange("p v j -> p (v j)"))
+        pick(1, 0)
+        pick(1, 1)
+        pick(2, 0)
+        pick(3, 0)
+        w3_grouped = sb([P, PACK, P, PACK], BF16, "w3_grouped", tag="w1_codes")
         w3_codes = sb([P, H], U32, "w3_codes")
         w3_plane = sb([P, H], U8, "w3_plane")
-        deal_weights(nc.vector.tensor_copy, w3_grouped, w3_raw, 0, W3_VECTOR_M)
-        deal_weights(nc.scalar.copy, w3_grouped, w3_raw, W3_VECTOR_M, P)
+        deal_weights(nc.scalar.copy, w3_grouped, w3_raw, 0, P)
         quantize(nc, w3_codes[:], w3_plane[:], w3_grouped[:].rearrange("p t m j -> p (t m j)"))
+        picked[1, 1] = sb([P, 2, V], F32, "picked11", tag="w1_codes")
+        pick(2, 1)
+        pick(3, 1)
+        a_grouped1 = sb([P, V, PACK], BF16, "a_grouped1", tag="w3_raw")
+        interleave(nc.scalar.copy, a_grouped1, a_raw[1])
+        a_codes.append(sb([P, V], U32, "a_codes1", tag="h3"))
+        quantize(nc, a_codes[1][:], a_plane[1][:], a_grouped1[:].rearrange("p v j -> p (v j)"))
 
-        f_banks = []
-        for d in range(D):
-            a_grouped = sb([P, V, PACK], BF16, "a_grouped%d" % d)
-            a_codes = sb([P, V], U32, "a_codes%d" % d)
-            a_plane = sb([P, V], U8, "a_plane%d" % d)
-            nc.scalar.copy(
-                out=a_grouped[:].rearrange("p (c i) j -> p c j i", i=4),
-                in_=a_raw[d][:].rearrange("p j (c i) -> p c j i", i=4),
-            )
-            quantize(nc, a_codes[:], a_plane[:], a_grouped[:].rearrange("p v j -> p (v j)"))
-            for pair in range(2):
-                bank = psum.tile([P, 2, V], F32, name="f_bank%d%d" % (d, pair), tag="bank%d" % (4 + 2 * d + pair))
-                for e in range(2):
-                    t = 2 * pair + e
-                    nc.tensor.matmul_mx(
-                        out=bank[:, e, :],
-                        lhsT=w3_codes[:, t * P:(t + 1) * P].bitcast(FP8X4),
-                        lhsT_scale=w3_plane[:, t * P:(t + 1) * P],
-                        rhs=a_codes[:].bitcast(FP8X4),
-                        rhs_scale=a_plane[:],
-                        start=True,
-                        stop=True,
-                    )
-                f_banks.append(bank)
-
-        picked = [sb([P, PACK, V], F32, "picked%d" % d) for d in range(D)]
-        for t in range(PACK):
-            for d in range(D):
-                nc.vector.tensor_copy(picked[d][:, t, :], h[t][:].indirect(pos_sb[d][:]))
         term = [sb([P, PACK, V], F32, "term%d" % d) for d in range(D)]
+        halves = [slice(u * P, (u + 1) * P) for u in range(V // P)]
         for d in range(D):
             for pair in range(2):
+                bank = psum.tile([P, 2, V], F32, name="f_bank%d%d" % (d, pair), tag="bank%d" % ((5 + 2 * d + pair) % 8))
+                for e in range(2):
+                    mx(bank[:, e, :], w3_codes, w3_plane, 2 * pair + e, a_codes[d], a_plane[d])
                 rows = slice(2 * pair, 2 * pair + 2)
-                nc.vector.tensor_tensor(term[d][:, rows, :], f_banks[2 * d + pair][:], picked[d][:, rows, :], MULT)
+                for cols in halves if (d, pair) == (1, 1) else [slice(0, V)]:
+                    nc.vector.tensor_tensor(term[d][:, rows, cols], bank[:, :, cols], picked[d, pair][:, :, cols], MULT)
 
         z_grouped = sb([P, V, PACK], BF16, "z_grouped")
         z_codes = sb([P, V], U32, "z_codes")
         z_plane = sb([P, V], U8, "z_plane")
-        nc.vector.tensor_tensor(
-            z_grouped[:].rearrange("p (c i) t -> p c t i", i=4),
-            term[0][:].rearrange("p t (c i) -> p c t i", i=4),
-            term[1][:].rearrange("p t (c i) -> p c t i", i=4),
-            ADD,
-        )
-        quantize(nc, z_codes[:], z_plane[:], z_grouped[:].rearrange("p v t -> p (v t)"))
-
-        for b in range(N // P):
-            bank = psum.tile([P, V], F32, name="out_bank%d" % b, tag="bank%d" % b)
-            nc.tensor.matmul_mx(
-                out=bank[:],
-                lhsT=w2_codes[:, 2 * b * P:2 * (b + 1) * P].bitcast(FP4X4),
-                lhsT_scale=w2_plane[:, b * P:(b + 1) * P],
-                rhs=z_codes[:].bitcast(FP8X4),
-                rhs_scale=z_plane[:],
-                start=True,
-                stop=True,
+        for cols in halves:
+            nc.vector.tensor_tensor(
+                z_grouped[:, cols, :].rearrange("p (c i) t -> p c t i", i=4),
+                term[0][:, :, cols].rearrange("p t (c i) -> p c t i", i=4),
+                term[1][:, :, cols].rearrange("p t (c i) -> p c t i", i=4),
+                ADD,
             )
-            result = sb([P, V], F32, "result%d" % b)
-            if b == 0:
+        for cols in halves:
+            quantize(nc, z_codes[:, cols], z_plane[:, cols], z_grouped[:, cols, :].rearrange("p v t -> p (v t)"))
+
+        out_rows = out.rearrange("(b p) v -> p b v", p=P)
+        for u, cols in enumerate(halves):
+            bank = psum.tile([P, N // P, P], F32, name="out_bank%d" % u, tag="bank%d" % (1 + u))
+            for b in range(N // P):
+                nc.tensor.matmul_mx(
+                    out=bank[:, b, :],
+                    lhsT=w2_codes[:, 2 * b * P:2 * (b + 1) * P].bitcast(FP4X4),
+                    lhsT_scale=w2_plane[:, b * P:(b + 1) * P],
+                    rhs=z_codes[:, cols].bitcast(FP8X4),
+                    rhs_scale=z_plane[:, cols],
+                    start=True,
+                    stop=True,
+                )
+            result = sb([P, N // P, P], F32, "result%d" % u)
+            if u == 0:
                 nc.scalar.copy(out=result[:], in_=bank[:])
-                nc.scalar.dma_start(out=out[b * P:(b + 1) * P, :], in_=result[:])
+                nc.scalar.dma_start(out=out_rows[:, :, cols], in_=result[:])
             else:
                 nc.vector.tensor_copy(out=result[:], in_=bank[:])
-                nc.sync.dma_start(out=out[b * P:(b + 1) * P, :], in_=result[:])
+                nc.sync.dma_start(out=out_rows[:, :, cols], in_=result[:])

@@ -21,13 +21,13 @@ ADD = mybir.AluOpType.add
 P = 128
 PACK = 4
 HALF = S // 2
-W1_SCALAR_M = 80
+W1_SCALAR_M = 76
 
 
-def deal_weights(copy, grouped, raw, m0, m1):
+def deal_weights(copy, grouped, raw, m0, m1, ts=slice(0, PACK)):
     copy(
-        out=grouped[:].rearrange("p t m j -> p m j t")[:, m0:m1],
-        in_=raw[:].rearrange("p j (m t) -> p m j t", t=PACK),
+        out=grouped[:].rearrange("p t m j -> p m j t")[:, m0:m1, :, ts],
+        in_=raw[:].rearrange("p j (m t) -> p m j t", t=PACK)[:, :, :, ts],
     )
 
 
@@ -73,12 +73,12 @@ def tile_picked_dime_none_e_kernel(tc, xT, aT, w1, w3, w2_words, w2_scales, offs
         nc.sync.dma_start(out=x_raw[0][:], in_=x_rows[:, 0, :])
         nc.sync.dma_start(offs_sb[:], offs)
         nc.sync.dma_start(out=x_raw[1][:], in_=x_rows[:, 1, :])
-        nc.sync.dma_start(pos_sb[0][:], pos1)
-        nc.sync.dma_start(pos_sb[1][:], pos2)
         nc.sync.dma_start(out=x_raw[2][:], in_=x_rows[:, 2, :])
         nc.sync.dma_start(out=x_raw[3][:], in_=x_rows[:, 3, :])
         nc.sync.dma_start(out=w1_raw_a[:], in_=w1_rows[:, :, :w1_cut])
         nc.sync.dma_start(out=w1_raw_b[:], in_=w1_rows[:, :, w1_cut:])
+        nc.sync.dma_start(pos_sb[0][:], pos1)
+        nc.sync.dma_start(pos_sb[1][:], pos2)
         nc.sync.dma_start(out=a_raw[0][:], in_=a_rows[:, :, :V])
         nc.sync.dma_start(out=w3_raw[:], in_=w3.rearrange("(p j) c -> p j c", j=PACK))
         nc.sync.dma_start(out=a_raw[1][:], in_=a_rows[:, :, V:])
@@ -87,19 +87,25 @@ def tile_picked_dime_none_e_kernel(tc, xT, aT, w1, w3, w2_words, w2_scales, offs
             nc.sync.dma_start(out=w2_plane[32 * q:32 * q + 4, :].bitcast(I32), in_=w2_scales[0, 4 * q:4 * q + 4, :].bitcast(I32))
 
         x_grouped = sb([P, S, PACK], BF16, "x_grouped")
-        for j in range(PACK):
+        entry_halves = [slice(u * HALF, (u + 1) * HALF) for u in range(2)]
+        for j in range(PACK - 1):
             nc.vector.tensor_copy(x_grouped[:, :, j], x_raw[j][:].indirect(offs_sb[:]))
-        x_plane = [sb([P, HALF], U8, "x_plane%d" % u) for u in range(2)]
-        x_codes = [sb([P, HALF], U32, "x_codes0")]
-        quantize(nc, x_codes[0][:], x_plane[0][:], x_grouped[:, :HALF, :].rearrange("p s j -> p (s j)"))
+        for cols in entry_halves:
+            nc.vector.tensor_copy(
+                x_grouped[:, cols, PACK - 1],
+                x_raw[PACK - 1][:].indirect(offs_sb[:, cols.start // 16:cols.stop // 16]),
+            )
+        x_plane = sb([P, S], U8, "x_plane")
+        x_codes = sb([P, S], U32, "x_codes")
+        for cols in entry_halves:
+            quantize(nc, x_codes[:, cols], x_plane[:, cols], x_grouped[:, cols, :].rearrange("p s j -> p (s j)"))
 
         w1_grouped = sb([P, PACK, P, PACK], BF16, "w1_grouped")
         w1_codes = sb([P, H], U32, "w1_codes")
         w1_plane = sb([P, H], U8, "w1_plane")
         deal_weights(nc.scalar.copy, w1_grouped, w1_raw_a, 0, W1_SCALAR_M)
-        deal_weights(nc.vector.tensor_copy, w1_grouped, w1_raw_b, W1_SCALAR_M, P)
-        x_codes.append(sb([P, HALF], U32, "x_codes1", tag="w1_raw_b"))
-        quantize(nc, x_codes[1][:], x_plane[1][:], x_grouped[:, HALF:, :].rearrange("p s j -> p (s j)"))
+        for pair in range(2):
+            deal_weights(nc.vector.tensor_copy, w1_grouped, w1_raw_b, W1_SCALAR_M, P, slice(2 * pair, 2 * pair + 2))
 
         def mx(bank, codes, plane, t, rhs_codes, rhs_plane, cols=slice(None)):
             nc.tensor.matmul_mx(
@@ -112,26 +118,30 @@ def tile_picked_dime_none_e_kernel(tc, xT, aT, w1, w3, w2_words, w2_scales, offs
                 stop=True,
             )
 
+        def quantize_w1(t0, t1):
+            cols = slice(t0 * P, t1 * P)
+            quantize(nc, w1_codes[:, cols], w1_plane[:, cols], w1_grouped[:, t0:t1].rearrange("p t m j -> p (t m j)"))
+
+        a_codes = [sb([P, V], U32, "a_codes%d" % d) for d in range(D)]
+        a_plane = [sb([P, V], U8, "a_plane%d" % d) for d in range(D)]
+        a_grouped0 = sb([P, V, PACK], BF16, "a_grouped0", tag="x_grouped")
+        quantize_w1(0, 1)
+        quantize_w1(1, 2)
+        interleave(nc.vector.tensor_copy, a_grouped0, a_raw[0])
+        quantize_w1(2, 4)
+
         h = [sb([P, S], F32, "h%d" % t) for t in range(PACK)]
-        for t in range(PACK):
-            cols = slice(t * P, (t + 1) * P)
-            quantize(nc, w1_codes[:, cols], w1_plane[:, cols], w1_grouped[:, t].rearrange("p m j -> p (m j)"))
         for t in range(PACK):
             if t == 0:
                 for u in range(2):
+                    cols = slice(u * HALF, (u + 1) * HALF)
                     bank = psum.tile([P, HALF], F32, name="h_bank0%d" % u, tag="bank%d" % u)
-                    mx(bank[:], w1_codes, w1_plane, t, x_codes[u], x_plane[u])
-                    nc.scalar.activation(out=h[t][:, u * HALF:(u + 1) * HALF], in_=bank[:], func=SILU)
+                    mx(bank[:], w1_codes, w1_plane, t, x_codes, x_plane, cols)
+                    nc.scalar.activation(out=h[t][:, cols], in_=bank[:], func=SILU)
             else:
                 bank = psum.tile([P, S], F32, name="h_bank%d" % t, tag="bank%d" % (t + 1))
-                for u in range(2):
-                    mx(bank[:, u * HALF:(u + 1) * HALF], w1_codes, w1_plane, t, x_codes[u], x_plane[u])
+                mx(bank[:], w1_codes, w1_plane, t, x_codes, x_plane)
                 nc.scalar.activation(out=h[t][:], in_=bank[:], func=SILU)
-
-        a_codes = []
-        a_plane = [sb([P, V], U8, "a_plane%d" % d) for d in range(D)]
-        a_grouped0 = sb([P, V, PACK], BF16, "a_grouped0", tag="x_grouped")
-        interleave(nc.vector.tensor_copy, a_grouped0, a_raw[0])
 
         picked = {}
 
@@ -141,9 +151,8 @@ def tile_picked_dime_none_e_kernel(tc, xT, aT, w1, w3, w2_words, w2_scales, offs
         for key in ((0, 0), (1, 0), (0, 1)):
             picked[key] = sb([P, 2, V], F32, "picked%d%d" % key)
         pick(0, 0)
-        pick(0, 1)
-        a_codes.append(sb([P, V], U32, "a_codes0", tag="h0"))
         quantize(nc, a_codes[0][:], a_plane[0][:], a_grouped0[:].rearrange("p v j -> p (v j)"))
+        pick(0, 1)
         pick(1, 0)
         pick(1, 1)
         pick(2, 0)
@@ -153,12 +162,11 @@ def tile_picked_dime_none_e_kernel(tc, xT, aT, w1, w3, w2_words, w2_scales, offs
         w3_plane = sb([P, H], U8, "w3_plane")
         deal_weights(nc.scalar.copy, w3_grouped, w3_raw, 0, P)
         quantize(nc, w3_codes[:], w3_plane[:], w3_grouped[:].rearrange("p t m j -> p (t m j)"))
-        picked[1, 1] = sb([P, 2, V], F32, "picked11", tag="w1_codes")
+        picked[1, 1] = sb([P, 2, V], F32, "picked11", tag="w3_raw")
         pick(2, 1)
         pick(3, 1)
-        a_grouped1 = sb([P, V, PACK], BF16, "a_grouped1", tag="w3_raw")
+        a_grouped1 = sb([P, V, PACK], BF16, "a_grouped1", tag="w1_plane")
         interleave(nc.scalar.copy, a_grouped1, a_raw[1])
-        a_codes.append(sb([P, V], U32, "a_codes1", tag="h3"))
         quantize(nc, a_codes[1][:], a_plane[1][:], a_grouped1[:].rearrange("p v j -> p (v j)"))
 
         term = [sb([P, PACK, V], F32, "term%d" % d) for d in range(D)]

@@ -143,42 +143,46 @@ def tile_picked_dime_none_e_kernel(tc, xT, aT, w1, w3, w2_words, w2_scales, offs
                 mx(bank[:], w1_codes, w1_plane, t, x_codes, x_plane)
                 nc.scalar.activation(out=h[t][:], in_=bank[:], func=SILU)
 
-        picked = {}
+        def pick(target, t, d):
+            nc.vector.tensor_copy(target, h[t][:].indirect(pos_sb[d][:]))
 
-        def pick(t, d):
-            nc.vector.tensor_copy(picked[d, t // 2][:, t % 2, :], h[t][:].indirect(pos_sb[d][:]))
-
-        for key in ((0, 0), (1, 0), (0, 1)):
-            picked[key] = sb([P, 2, V], F32, "picked%d%d" % key)
-        pick(0, 0)
+        picked = [sb([P, PACK, V], F32, "picked0"), sb([P, 2, V], F32, "picked1")]
+        pick(picked[0][:, 0, :], 0, 0)
         quantize(nc, a_codes[0][:], a_plane[0][:], a_grouped0[:].rearrange("p v j -> p (v j)"))
-        pick(0, 1)
-        pick(1, 0)
-        pick(1, 1)
-        pick(2, 0)
-        pick(3, 0)
+        pick(picked[1][:, 0, :], 0, 1)
+        pick(picked[0][:, 1, :], 1, 0)
+        pick(picked[1][:, 1, :], 1, 1)
+        pick(picked[0][:, 2, :], 2, 0)
+        pick(picked[0][:, 3, :], 3, 0)
+
         w3_grouped = sb([P, PACK, P, PACK], BF16, "w3_grouped", tag="w1_codes")
         w3_codes = sb([P, H], U32, "w3_codes")
         w3_plane = sb([P, H], U8, "w3_plane")
         deal_weights(nc.scalar.copy, w3_grouped, w3_raw, 0, P)
         quantize(nc, w3_codes[:], w3_plane[:], w3_grouped[:].rearrange("p t m j -> p (t m j)"))
-        picked[1, 1] = sb([P, 2, V], F32, "picked11", tag="w3_raw")
-        pick(2, 1)
-        pick(3, 1)
+        picked12 = sb([P, V], F32, "picked12", tag="w3_raw")
+        pick(picked12[:], 2, 1)
         a_grouped1 = sb([P, V, PACK], BF16, "a_grouped1", tag="w1_plane")
         interleave(nc.scalar.copy, a_grouped1, a_raw[1])
         quantize(nc, a_codes[1][:], a_plane[1][:], a_grouped1[:].rearrange("p v j -> p (v j)"))
+        picked_last = sb([P, V], F32, "picked_last", tag="a_raw1")
+        pick(picked_last[:], 3, 1)
 
-        term = [sb([P, PACK, V], F32, "term%d" % d) for d in range(D)]
+        term = [sb([P, PACK, V], F32, "term0", tag="w1_plane"), sb([P, PACK, V], F32, "term1")]
         halves = [slice(u * P, (u + 1) * P) for u in range(V // P)]
-        for d in range(D):
-            for pair in range(2):
-                bank = psum.tile([P, 2, V], F32, name="f_bank%d%d" % (d, pair), tag="bank%d" % ((5 + 2 * d + pair) % 8))
-                for e in range(2):
-                    mx(bank[:, e, :], w3_codes, w3_plane, 2 * pair + e, a_codes[d], a_plane[d])
-                rows = slice(2 * pair, 2 * pair + 2)
-                for cols in halves if (d, pair) == (1, 1) else [slice(0, V)]:
-                    nc.vector.tensor_tensor(term[d][:, rows, cols], bank[:, :, cols], picked[d, pair][:, :, cols], MULT)
+        f_bank = {}
+        for n, (d, pair) in enumerate(((0, 0), (0, 1), (1, 1), (1, 0))):
+            f_bank[d, pair] = psum.tile([P, 2, V], F32, name="f_bank%d%d" % (d, pair), tag="bank%d" % ((5 + n) % 8))
+            for e in range(2):
+                mx(f_bank[d, pair][:, e, :], w3_codes, w3_plane, 2 * pair + e, a_codes[d], a_plane[d])
+        filters = sb([P, 2, V], F32, "filters")
+        nc.scalar.copy(out=filters[:], in_=f_bank[0, 0][:])
+        nc.gpsimd.tensor_tensor(term[0][:, 0:2, :], filters[:], picked[0][:, 0:2, :], MULT)
+        nc.vector.tensor_tensor(term[0][:, 2:, :], f_bank[0, 1][:], picked[0][:, 2:, :], MULT)
+        nc.vector.tensor_tensor(term[1][:, 2, :], f_bank[1, 1][:, 0, :], picked12[:], MULT)
+        nc.vector.tensor_tensor(term[1][:, 3, :], f_bank[1, 1][:, 1, :], picked_last[:], MULT)
+        for cols in halves:
+            nc.vector.tensor_tensor(term[1][:, 0:2, cols], f_bank[1, 0][:, :, cols], picked[1][:, 0:2, cols], MULT)
 
         z_grouped = sb([P, V, PACK], BF16, "z_grouped")
         z_codes = sb([P, V], U32, "z_codes")

@@ -20,26 +20,28 @@ ADD = mybir.AluOpType.add
 
 P = 128
 PACK = 4
-HALF = S // 2
-W1_SCALAR_M = 76
+LINE = 4
+LIST_COLUMN = 16
+QUADRANT = 32
+W1_CUT = 28
 
 
-def deal_weights(copy, grouped, raw, m0, m1, ts=slice(0, PACK)):
+def deal_weights(copy, grouped, raw, ts, ms):
     copy(
-        out=grouped[:].rearrange("p t m j -> p m j t")[:, m0:m1, :, ts],
-        in_=raw[:].rearrange("p j (m t) -> p m j t", t=PACK)[:, :, :, ts],
+        out=grouped[:].rearrange("p t m j -> p m j t")[:, ms, :, ts],
+        in_=raw[:].rearrange("p j (m t) -> p m j t", t=PACK)[:, ms, :, ts],
     )
 
 
 def interleave(copy, grouped, raw):
     copy(
-        out=grouped[:].rearrange("p (c i) j -> p c j i", i=4),
-        in_=raw[:].rearrange("p j (c i) -> p c j i", i=4),
+        out=grouped[:].rearrange("p (c i) j -> p c j i", i=LINE),
+        in_=raw[:].rearrange("p j (c i) -> p c j i", i=LINE),
     )
 
 
-def quantize(nc, codes, scales, grouped):
-    nc.vector.quantize_mx(out=codes.bitcast(FP8X4), scales=scales, in_=grouped)
+def quantize(nc, codes, plane, grouped):
+    nc.vector.quantize_mx(out=codes.bitcast(FP8X4), scales=plane, in_=grouped)
 
 
 def tile_picked_dime_none_e_kernel(tc, xT, aT, w1, w3, w2_words, w2_scales, offs, pos1, pos2, out):
@@ -51,76 +53,75 @@ def tile_picked_dime_none_e_kernel(tc, xT, aT, w1, w3, w2_words, w2_scales, offs
         def sb(shape, dtype, name, tag=None):
             return keep.tile(shape, dtype, name=name, tag=tag or name, align_bytes=64)
 
-        offs_sb = sb([P, S // 16], U16, "offs_sb")
-        pos_sb = [sb([P, V // 16], U16, "pos%d_sb" % d) for d in range(D)]
-        w1_cut = PACK * W1_SCALAR_M
-        w1_raw_a = sb([P, PACK, w1_cut], F32, "w1_raw_a")
-        w1_raw_b = sb([P, PACK, H - w1_cut], F32, "w1_raw_b")
+        offs_sb = sb([P, S // LIST_COLUMN], U16, "offs_sb")
+        pos_sb = [sb([P, V // LIST_COLUMN], U16, "pos%d_sb" % d) for d in range(D)]
+        w1_raw = sb([P, PACK, H], F32, "w1_raw")
         w3_raw = sb([P, PACK, H], F32, "w3_raw")
         x_raw = [sb([P, T], F32, "x_raw%d" % j) for j in range(PACK)]
         a_raw = [sb([P, PACK, V], F32, "a_raw%d" % d) for d in range(D)]
         w2_codes = sb([P, 2 * N], U8, "w2_codes")
         w2_plane = sb([P, N], U8, "w2_plane")
-        warm = sb([P, 2], F32, "warm")
+        zeros = sb([P, 2], F32, "zeros")
 
-        nc.vector.memset(warm[:, 0:1], 0.0)
+        nc.vector.memset(zeros[:, 0:1], 0.0)
         nc.vector.memset(w2_plane[:].bitcast(I32), 0)
-        nc.scalar.activation(out=warm[:, 1:2], in_=warm[:, 0:1], func=SILU)
+        zero_bias = zeros[:, 1:2]
+        nc.scalar.activation(out=zero_bias, in_=zeros[:, 0:1], func=SILU)
 
         x_rows = xT.rearrange("(p j) t -> p j t", j=PACK)
         a_rows = aT.rearrange("(p j) u -> p j u", j=PACK)
-        w1_rows = w1.rearrange("(p j) c -> p j c", j=PACK)
         nc.sync.dma_start(out=x_raw[0][:], in_=x_rows[:, 0, :])
         nc.sync.dma_start(offs_sb[:], offs)
-        nc.sync.dma_start(out=x_raw[1][:], in_=x_rows[:, 1, :])
-        nc.sync.dma_start(out=x_raw[2][:], in_=x_rows[:, 2, :])
-        nc.sync.dma_start(out=x_raw[3][:], in_=x_rows[:, 3, :])
-        nc.sync.dma_start(out=w1_raw_a[:], in_=w1_rows[:, :, :w1_cut])
-        nc.sync.dma_start(out=w1_raw_b[:], in_=w1_rows[:, :, w1_cut:])
+        for j in range(1, PACK):
+            nc.sync.dma_start(out=x_raw[j][:], in_=x_rows[:, j, :])
+        nc.sync.dma_start(out=w1_raw[:], in_=w1.rearrange("(p j) c -> p j c", j=PACK))
+        nc.sync.dma_start(out=a_raw[0][:], in_=a_rows[:, :, :V])
         nc.sync.dma_start(pos_sb[0][:], pos1)
         nc.sync.dma_start(pos_sb[1][:], pos2)
-        nc.sync.dma_start(out=a_raw[0][:], in_=a_rows[:, :, :V])
         nc.sync.dma_start(out=w3_raw[:], in_=w3.rearrange("(p j) c -> p j c", j=PACK))
         nc.sync.dma_start(out=a_raw[1][:], in_=a_rows[:, :, V:])
         nc.sync.dma_start(out=w2_codes[:].bitcast(I32), in_=w2_words[0].bitcast(I32))
-        for q in range(4):
-            nc.sync.dma_start(out=w2_plane[32 * q:32 * q + 4, :].bitcast(I32), in_=w2_scales[0, 4 * q:4 * q + 4, :].bitcast(I32))
+        for q in range(P // QUADRANT):
+            nc.sync.dma_start(
+                out=w2_plane[QUADRANT * q:QUADRANT * q + 4, :].bitcast(I32),
+                in_=w2_scales[0, 4 * q:4 * q + 4, :].bitcast(I32),
+            )
 
         x_grouped = sb([P, S, PACK], BF16, "x_grouped")
-        entry_halves = [slice(u * HALF, (u + 1) * HALF) for u in range(2)]
+        entry_halves = [slice(u * S // 2, (u + 1) * S // 2) for u in range(2)]
         for j in range(PACK - 1):
             nc.vector.tensor_copy(x_grouped[:, :, j], x_raw[j][:].indirect(offs_sb[:]))
-        for cols in entry_halves:
+        for entries in entry_halves:
             nc.vector.tensor_copy(
-                x_grouped[:, cols, PACK - 1],
-                x_raw[PACK - 1][:].indirect(offs_sb[:, cols.start // 16:cols.stop // 16]),
+                x_grouped[:, entries, PACK - 1],
+                x_raw[PACK - 1][:].indirect(offs_sb[:, entries.start // LIST_COLUMN:entries.stop // LIST_COLUMN]),
             )
         x_plane = sb([P, S], U8, "x_plane")
         x_codes = sb([P, S], U32, "x_codes")
-        for cols in entry_halves:
-            quantize(nc, x_codes[:, cols], x_plane[:, cols], x_grouped[:, cols, :].rearrange("p s j -> p (s j)"))
+        for entries in entry_halves:
+            quantize(nc, x_codes[:, entries], x_plane[:, entries], x_grouped[:, entries, :].rearrange("p s j -> p (s j)"))
 
         w1_grouped = sb([P, PACK, P, PACK], BF16, "w1_grouped")
         w1_codes = sb([P, H], U32, "w1_codes")
         w1_plane = sb([P, H], U8, "w1_plane")
-        deal_weights(nc.scalar.copy, w1_grouped, w1_raw_a, 0, W1_SCALAR_M)
-        for pair in range(2):
-            deal_weights(nc.vector.tensor_copy, w1_grouped, w1_raw_b, W1_SCALAR_M, P, slice(2 * pair, 2 * pair + 2))
+        deal_weights(nc.vector.tensor_copy, w1_grouped, w1_raw, slice(0, 2), slice(0, P))
+        deal_weights(nc.vector.tensor_copy, w1_grouped, w1_raw, slice(2, 4), slice(0, W1_CUT))
+        deal_weights(nc.scalar.copy, w1_grouped, w1_raw, slice(2, 4), slice(W1_CUT, P))
 
-        def mx(bank, codes, plane, t, rhs_codes, rhs_plane, cols=slice(None)):
+        def hidden_tile(bank, w_codes, w_plane, t, codes, plane):
             nc.tensor.matmul_mx(
                 out=bank,
-                lhsT=codes[:, t * P:(t + 1) * P].bitcast(FP8X4),
-                lhsT_scale=plane[:, t * P:(t + 1) * P],
-                rhs=rhs_codes[:, cols].bitcast(FP8X4),
-                rhs_scale=rhs_plane[:, cols],
+                lhsT=w_codes[:, t * P:(t + 1) * P].bitcast(FP8X4),
+                lhsT_scale=w_plane[:, t * P:(t + 1) * P],
+                rhs=codes.bitcast(FP8X4),
+                rhs_scale=plane,
                 start=True,
                 stop=True,
             )
 
         def quantize_w1(t0, t1):
-            cols = slice(t0 * P, t1 * P)
-            quantize(nc, w1_codes[:, cols], w1_plane[:, cols], w1_grouped[:, t0:t1].rearrange("p t m j -> p (t m j)"))
+            columns = slice(t0 * P, t1 * P)
+            quantize(nc, w1_codes[:, columns], w1_plane[:, columns], w1_grouped[:, t0:t1].rearrange("p t m j -> p (t m j)"))
 
         a_codes = [sb([P, V], U32, "a_codes%d" % d) for d in range(D)]
         a_plane = [sb([P, V], U8, "a_plane%d" % d) for d in range(D)]
@@ -131,89 +132,83 @@ def tile_picked_dime_none_e_kernel(tc, xT, aT, w1, w3, w2_words, w2_scales, offs
         quantize_w1(2, 4)
 
         h = [sb([P, S], F32, "h%d" % t) for t in range(PACK)]
-        for t in range(PACK):
-            if t == 0:
-                for u in range(2):
-                    cols = slice(u * HALF, (u + 1) * HALF)
-                    bank = psum.tile([P, HALF], F32, name="h_bank0%d" % u, tag="bank%d" % u)
-                    mx(bank[:], w1_codes, w1_plane, t, x_codes, x_plane, cols)
-                    nc.scalar.activation(out=h[t][:, cols], in_=bank[:], func=SILU)
-            else:
-                bank = psum.tile([P, S], F32, name="h_bank%d" % t, tag="bank%d" % (t + 1))
-                mx(bank[:], w1_codes, w1_plane, t, x_codes, x_plane)
-                nc.scalar.activation(out=h[t][:], in_=bank[:], func=SILU)
+        for u, entries in enumerate(entry_halves):
+            bank = psum.tile([P, S // 2], F32, name="h_bank0%d" % u, tag="bank%d" % u)
+            hidden_tile(bank[:], w1_codes, w1_plane, 0, x_codes[:, entries], x_plane[:, entries])
+            nc.scalar.activation(out=h[0][:, entries], in_=bank[:], func=SILU, bias=zero_bias)
+        for t in range(1, PACK):
+            bank = psum.tile([P, S], F32, name="h_bank%d" % t, tag="bank%d" % (t + 1))
+            hidden_tile(bank[:], w1_codes, w1_plane, t, x_codes[:, :], x_plane[:, :])
+            nc.scalar.activation(out=h[t][:], in_=bank[:], func=SILU, bias=zero_bias)
 
         def pick(target, t, d):
             nc.vector.tensor_copy(target, h[t][:].indirect(pos_sb[d][:]))
 
-        picked = [sb([P, PACK, V], F32, "picked0"), sb([P, 2, V], F32, "picked1")]
-        pick(picked[0][:, 0, :], 0, 0)
+        picked0 = sb([P, PACK, V], F32, "picked0")
+        picked1_low = sb([P, 2, V], F32, "picked1_low")
+        pick(picked0[:, 0, :], 0, 0)
         quantize(nc, a_codes[0][:], a_plane[0][:], a_grouped0[:].rearrange("p v j -> p (v j)"))
-        pick(picked[1][:, 0, :], 0, 1)
-        pick(picked[0][:, 1, :], 1, 0)
-        pick(picked[1][:, 1, :], 1, 1)
-        pick(picked[0][:, 2, :], 2, 0)
-        pick(picked[0][:, 3, :], 3, 0)
+        pick(picked1_low[:, 0, :], 0, 1)
+        pick(picked0[:, 1, :], 1, 0)
+        pick(picked1_low[:, 1, :], 1, 1)
+        pick(picked0[:, 2, :], 2, 0)
+        pick(picked0[:, 3, :], 3, 0)
 
         w3_grouped = sb([P, PACK, P, PACK], BF16, "w3_grouped", tag="w1_codes")
         w3_codes = sb([P, H], U32, "w3_codes")
         w3_plane = sb([P, H], U8, "w3_plane")
-        deal_weights(nc.scalar.copy, w3_grouped, w3_raw, 0, P)
+        deal_weights(nc.scalar.copy, w3_grouped, w3_raw, slice(0, PACK), slice(0, P))
         quantize(nc, w3_codes[:], w3_plane[:], w3_grouped[:].rearrange("p t m j -> p (t m j)"))
-        picked12 = sb([P, V], F32, "picked12", tag="w3_raw")
-        pick(picked12[:], 2, 1)
+        picked1_tile2 = sb([P, V], F32, "picked1_tile2", tag="w3_raw")
+        pick(picked1_tile2[:], 2, 1)
         a_grouped1 = sb([P, V, PACK], BF16, "a_grouped1", tag="w1_plane")
         interleave(nc.scalar.copy, a_grouped1, a_raw[1])
         quantize(nc, a_codes[1][:], a_plane[1][:], a_grouped1[:].rearrange("p v j -> p (v j)"))
-        picked_last = sb([P, V], F32, "picked_last", tag="a_raw1")
-        pick(picked_last[:], 3, 1)
+        picked1_tile3 = sb([P, V], F32, "picked1_tile3", tag="a_raw1")
+        pick(picked1_tile3[:], 3, 1)
 
         term = [sb([P, PACK, V], F32, "term0", tag="w1_plane"), sb([P, PACK, V], F32, "term1")]
-        halves = [slice(u * P, (u + 1) * P) for u in range(V // P)]
+        target_halves = [slice(u * P, (u + 1) * P) for u in range(V // P)]
         f_bank = {}
         for n, (d, pair) in enumerate(((0, 0), (0, 1), (1, 1), (1, 0))):
             f_bank[d, pair] = psum.tile([P, 2, V], F32, name="f_bank%d%d" % (d, pair), tag="bank%d" % ((5 + n) % 8))
             for e in range(2):
-                mx(f_bank[d, pair][:, e, :], w3_codes, w3_plane, 2 * pair + e, a_codes[d], a_plane[d])
+                hidden_tile(f_bank[d, pair][:, e, :], w3_codes, w3_plane, 2 * pair + e, a_codes[d][:, :], a_plane[d][:, :])
         filters = sb([P, 2, V], F32, "filters")
         nc.scalar.copy(out=filters[:], in_=f_bank[0, 0][:])
-        nc.gpsimd.tensor_tensor(term[0][:, 0:2, :], filters[:], picked[0][:, 0:2, :], MULT)
-        nc.vector.tensor_tensor(term[0][:, 2:, :], f_bank[0, 1][:], picked[0][:, 2:, :], MULT)
-        nc.vector.tensor_tensor(term[1][:, 2, :], f_bank[1, 1][:, 0, :], picked12[:], MULT)
-        nc.vector.tensor_tensor(term[1][:, 3, :], f_bank[1, 1][:, 1, :], picked_last[:], MULT)
-        for cols in halves:
-            nc.vector.tensor_tensor(term[1][:, 0:2, cols], f_bank[1, 0][:, :, cols], picked[1][:, 0:2, cols], MULT)
+        nc.gpsimd.tensor_tensor(term[0][:, 0:2, :], filters[:], picked0[:, 0:2, :], MULT)
+        nc.vector.tensor_tensor(term[0][:, 2:, :], f_bank[0, 1][:], picked0[:, 2:, :], MULT)
+        nc.vector.tensor_tensor(term[1][:, 2, :], f_bank[1, 1][:, 0, :], picked1_tile2[:], MULT)
+        nc.vector.tensor_tensor(term[1][:, 3, :], f_bank[1, 1][:, 1, :], picked1_tile3[:], MULT)
+        for targets in target_halves:
+            nc.vector.tensor_tensor(term[1][:, 0:2, targets], f_bank[1, 0][:, :, targets], picked1_low[:, 0:2, targets], MULT)
 
         z_grouped = sb([P, V, PACK], BF16, "z_grouped")
         z_codes = sb([P, V], U32, "z_codes")
         z_plane = sb([P, V], U8, "z_plane")
-        for cols in halves:
+        for targets in target_halves:
             nc.vector.tensor_tensor(
-                z_grouped[:, cols, :].rearrange("p (c i) t -> p c t i", i=4),
-                term[0][:, :, cols].rearrange("p t (c i) -> p c t i", i=4),
-                term[1][:, :, cols].rearrange("p t (c i) -> p c t i", i=4),
+                z_grouped[:, targets, :].rearrange("p (c i) t -> p c t i", i=LINE),
+                term[0][:, :, targets].rearrange("p t (c i) -> p c t i", i=LINE),
+                term[1][:, :, targets].rearrange("p t (c i) -> p c t i", i=LINE),
                 ADD,
             )
-        for cols in halves:
-            quantize(nc, z_codes[:, cols], z_plane[:, cols], z_grouped[:, cols, :].rearrange("p v t -> p (v t)"))
+        for targets in target_halves:
+            quantize(nc, z_codes[:, targets], z_plane[:, targets], z_grouped[:, targets, :].rearrange("p v t -> p (v t)"))
 
-        out_rows = out.rearrange("(b p) v -> p b v", p=P)
-        for u, cols in enumerate(halves):
-            bank = psum.tile([P, N // P, P], F32, name="out_bank%d" % u, tag="bank%d" % (1 + u))
-            for b in range(N // P):
+        result = [sb([P, V], F32, "result%d" % b) for b in range(N // P)]
+        for u, targets in enumerate(target_halves):
+            for b, copy in enumerate((nc.scalar.copy, nc.vector.tensor_copy)):
+                bank = psum.tile([P, P], F32, name="out_bank%d%d" % (u, b), tag="bank%d" % (1 + 2 * u + b))
                 nc.tensor.matmul_mx(
-                    out=bank[:, b, :],
+                    out=bank[:],
                     lhsT=w2_codes[:, 2 * b * P:2 * (b + 1) * P].bitcast(FP4X4),
                     lhsT_scale=w2_plane[:, b * P:(b + 1) * P],
-                    rhs=z_codes[:, cols].bitcast(FP8X4),
-                    rhs_scale=z_plane[:, cols],
+                    rhs=z_codes[:, targets].bitcast(FP8X4),
+                    rhs_scale=z_plane[:, targets],
                     start=True,
                     stop=True,
                 )
-            result = sb([P, N // P, P], F32, "result%d" % u)
-            if u == 0:
-                nc.scalar.copy(out=result[:], in_=bank[:])
-                nc.scalar.dma_start(out=out_rows[:, :, cols], in_=result[:])
-            else:
-                nc.vector.tensor_copy(out=result[:], in_=bank[:])
-                nc.sync.dma_start(out=out_rows[:, :, cols], in_=result[:])
+                copy(out=result[b][:, targets], in_=bank[:])
+        nc.scalar.dma_start(out=out[0:P, :], in_=result[0][:])
+        nc.sync.dma_start(out=out[P:N, :], in_=result[1][:])

@@ -23,20 +23,20 @@ PACK = 4
 LINE = 4
 LIST_COLUMN = 16
 QUADRANT = 32
-W1_CUT = 28
+W1_CUTS = (60, 68)
 
 
-def deal_weights(copy, grouped, raw, ts, ms):
+def deal_weights(copy, grouped, raw, pair, ms):
     copy(
-        out=grouped[:].rearrange("p t m j -> p m j t")[:, ms, :, ts],
-        in_=raw[:].rearrange("p j (m t) -> p m j t", t=PACK)[:, ms, :, ts],
+        out=grouped[:].rearrange("p e m j -> p m j e")[:, ms],
+        in_=raw[:].rearrange("p j (m t) -> p m j t", t=PACK)[:, ms, :, 2 * pair:2 * pair + 2],
     )
 
 
-def interleave(copy, grouped, raw):
+def interleave(copy, grouped, raw, targets):
     copy(
-        out=grouped[:].rearrange("p (c i) j -> p c j i", i=LINE),
-        in_=raw[:].rearrange("p j (c i) -> p c j i", i=LINE),
+        out=grouped[:, targets, :].rearrange("p (c i) j -> p c j i", i=LINE),
+        in_=raw[:, :, targets].rearrange("p j (c i) -> p c j i", i=LINE),
     )
 
 
@@ -101,12 +101,12 @@ def tile_picked_dime_none_e_kernel(tc, xT, aT, w1, w3, w2_words, w2_scales, offs
         for entries in entry_halves:
             quantize(nc, x_codes[:, entries], x_plane[:, entries], x_grouped[:, entries, :].rearrange("p s j -> p (s j)"))
 
-        w1_grouped = sb([P, PACK, P, PACK], BF16, "w1_grouped")
+        w1_grouped = [sb([P, 2, P, PACK], BF16, "w1_grouped%d" % pair) for pair in range(2)]
         w1_codes = sb([P, H], U32, "w1_codes")
         w1_plane = sb([P, H], U8, "w1_plane")
-        deal_weights(nc.vector.tensor_copy, w1_grouped, w1_raw, slice(0, 2), slice(0, P))
-        deal_weights(nc.vector.tensor_copy, w1_grouped, w1_raw, slice(2, 4), slice(0, W1_CUT))
-        deal_weights(nc.scalar.copy, w1_grouped, w1_raw, slice(2, 4), slice(W1_CUT, P))
+        for pair, cut in enumerate(W1_CUTS):
+            deal_weights(nc.scalar.copy, w1_grouped[pair], w1_raw, pair, slice(0, cut))
+            deal_weights(nc.vector.tensor_copy, w1_grouped[pair], w1_raw, pair, slice(cut, P))
 
         def hidden_tile(bank, w_codes, w_plane, t, codes, plane):
             nc.tensor.matmul_mx(
@@ -121,14 +121,14 @@ def tile_picked_dime_none_e_kernel(tc, xT, aT, w1, w3, w2_words, w2_scales, offs
 
         def quantize_w1(t0, t1):
             columns = slice(t0 * P, t1 * P)
-            quantize(nc, w1_codes[:, columns], w1_plane[:, columns], w1_grouped[:, t0:t1].rearrange("p t m j -> p (t m j)"))
+            quantize(nc, w1_codes[:, columns], w1_plane[:, columns], w1_grouped[t0 // 2][:, t0 % 2:(t1 - 1) % 2 + 1].rearrange("p e m j -> p (e m j)"))
 
         a_codes = [sb([P, V], U32, "a_codes%d" % d) for d in range(D)]
         a_plane = [sb([P, V], U8, "a_plane%d" % d) for d in range(D)]
         a_grouped0 = sb([P, V, PACK], BF16, "a_grouped0", tag="x_grouped")
         quantize_w1(0, 1)
         quantize_w1(1, 2)
-        interleave(nc.vector.tensor_copy, a_grouped0, a_raw[0])
+        interleave(nc.vector.tensor_copy, a_grouped0, a_raw[0], slice(0, V))
         quantize_w1(2, 4)
 
         h = [sb([P, S], F32, "h%d" % t) for t in range(PACK)]
@@ -141,47 +141,58 @@ def tile_picked_dime_none_e_kernel(tc, xT, aT, w1, w3, w2_words, w2_scales, offs
             hidden_tile(bank[:], w1_codes, w1_plane, t, x_codes[:, :], x_plane[:, :])
             nc.scalar.activation(out=h[t][:], in_=bank[:], func=SILU, bias=zero_bias)
 
-        def pick(target, t, d):
-            nc.vector.tensor_copy(target, h[t][:].indirect(pos_sb[d][:]))
+        picked = [sb([P, 2, V], F32, "picked0")]
 
-        picked0 = sb([P, PACK, V], F32, "picked0")
-        picked1_low = sb([P, 2, V], F32, "picked1_low")
-        pick(picked0[:, 0, :], 0, 0)
-        quantize(nc, a_codes[0][:], a_plane[0][:], a_grouped0[:].rearrange("p v j -> p (v j)"))
-        pick(picked1_low[:, 0, :], 0, 1)
-        pick(picked0[:, 1, :], 1, 0)
-        pick(picked1_low[:, 1, :], 1, 1)
-        pick(picked0[:, 2, :], 2, 0)
-        pick(picked0[:, 3, :], 3, 0)
+        def pick(t):
+            nc.vector.tensor_copy(picked[t // 2][:, t % 2, :], h[t][:].indirect(pos_sb[1][:]))
 
-        w3_grouped = sb([P, PACK, P, PACK], BF16, "w3_grouped", tag="w1_codes")
+        w3_grouped = [sb([P, 2, P, PACK], BF16, "w3_grouped%d" % pair) for pair in range(2)]
         w3_codes = sb([P, H], U32, "w3_codes")
         w3_plane = sb([P, H], U8, "w3_plane")
-        deal_weights(nc.scalar.copy, w3_grouped, w3_raw, slice(0, PACK), slice(0, P))
-        quantize(nc, w3_codes[:], w3_plane[:], w3_grouped[:].rearrange("p t m j -> p (t m j)"))
-        picked1_tile2 = sb([P, V], F32, "picked1_tile2", tag="w3_raw")
-        pick(picked1_tile2[:], 2, 1)
-        a_grouped1 = sb([P, V, PACK], BF16, "a_grouped1", tag="w1_plane")
-        interleave(nc.scalar.copy, a_grouped1, a_raw[1])
-        quantize(nc, a_codes[1][:], a_plane[1][:], a_grouped1[:].rearrange("p v j -> p (v j)"))
-        picked1_tile3 = sb([P, V], F32, "picked1_tile3", tag="a_raw1")
-        pick(picked1_tile3[:], 3, 1)
 
-        term = [sb([P, PACK, V], F32, "term0", tag="w1_plane"), sb([P, PACK, V], F32, "term1")]
-        target_halves = [slice(u * P, (u + 1) * P) for u in range(V // P)]
+        def quantize_w3(pair):
+            columns = slice(2 * pair * P, 2 * (pair + 1) * P)
+            quantize(nc, w3_codes[:, columns], w3_plane[:, columns], w3_grouped[pair][:].rearrange("p e m j -> p (e m j)"))
+
         f_bank = {}
-        for n, (d, pair) in enumerate(((0, 0), (0, 1), (1, 1), (1, 0))):
-            f_bank[d, pair] = psum.tile([P, 2, V], F32, name="f_bank%d%d" % (d, pair), tag="bank%d" % ((5 + n) % 8))
+
+        def filter_pair(d, pair):
+            f_bank[d, pair] = psum.tile([P, 2, V], F32, name="f_bank%d%d" % (d, pair), tag="bank%d" % ((5 + 2 * d + pair) % 8))
             for e in range(2):
                 hidden_tile(f_bank[d, pair][:, e, :], w3_codes, w3_plane, 2 * pair + e, a_codes[d][:, :], a_plane[d][:, :])
-        filters = sb([P, 2, V], F32, "filters")
-        nc.scalar.copy(out=filters[:], in_=f_bank[0, 0][:])
-        nc.gpsimd.tensor_tensor(term[0][:, 0:2, :], filters[:], picked0[:, 0:2, :], MULT)
-        nc.vector.tensor_tensor(term[0][:, 2:, :], f_bank[0, 1][:], picked0[:, 2:, :], MULT)
-        nc.vector.tensor_tensor(term[1][:, 2, :], f_bank[1, 1][:, 0, :], picked1_tile2[:], MULT)
-        nc.vector.tensor_tensor(term[1][:, 3, :], f_bank[1, 1][:, 1, :], picked1_tile3[:], MULT)
+
+        quantize(nc, a_codes[0][:], a_plane[0][:], a_grouped0[:].rearrange("p v j -> p (v j)"))
+        pick(0)
+        pick(1)
+        deal_weights(nc.vector.tensor_copy, w3_grouped[0], w3_raw, 0, slice(0, P))
+        deal_weights(nc.vector.tensor_copy, w3_grouped[1], w3_raw, 1, slice(0, P))
+        quantize_w3(0)
+        filter_pair(0, 0)
+        quantize_w3(1)
+        filter_pair(0, 1)
+        picked.append(sb([P, 2, V], F32, "picked1", tag="w3_raw"))
+        pick(2)
+        pick(3)
+        a_grouped1 = sb([P, V, PACK], BF16, "a_grouped1", tag="w1_plane")
+        interleave(nc.scalar.copy, a_grouped1, a_raw[1], slice(0, V))
+        filters = sb([P, PACK, V], F32, "filters")
+        for pair in range(2):
+            nc.scalar.copy(out=filters[:, 2 * pair:2 * pair + 2, :], in_=f_bank[0, pair][:])
+
+        term = [sb([P, PACK, V], F32, "term%d" % d) for d in range(D)]
+
+        def pick_times_filter(t):
+            nc.vector.tensor_tensor(term[0][:, t, :], h[t][:].indirect(pos_sb[0][:]), filters[:, t, :], MULT)
+
+        quantize(nc, a_codes[1][:], a_plane[1][:], a_grouped1[:].rearrange("p v j -> p (v j)"))
+        filter_pair(1, 0)
+        filter_pair(1, 1)
+        for t in range(PACK):
+            pick_times_filter(t)
+        target_halves = [slice(u * P, (u + 1) * P) for u in range(V // P)]
+        nc.vector.tensor_tensor(term[1][:, 0:2, :], f_bank[1, 0][:], picked[0][:], MULT)
         for targets in target_halves:
-            nc.vector.tensor_tensor(term[1][:, 0:2, targets], f_bank[1, 0][:, :, targets], picked1_low[:, 0:2, targets], MULT)
+            nc.vector.tensor_tensor(term[1][:, 2:, targets], f_bank[1, 1][:, :, targets], picked[1][:, :, targets], MULT)
 
         z_grouped = sb([P, V, PACK], BF16, "z_grouped")
         z_codes = sb([P, V], U32, "z_codes")

@@ -24,6 +24,7 @@ LINE = 4
 LIST_COLUMN = 16
 QUADRANT = 32
 W1_CUTS = (60, 68)
+W3_CUT = 44
 
 
 def deal_weights(copy, grouped, raw, pair, ms):
@@ -76,10 +77,10 @@ def tile_picked_dime_none_e_kernel(tc, xT, aT, w1, w3, w2_words, w2_scales, offs
             nc.sync.dma_start(out=x_raw[j][:], in_=x_rows[:, j, :])
         nc.sync.dma_start(out=w1_raw[:], in_=w1.rearrange("(p j) c -> p j c", j=PACK))
         nc.sync.dma_start(out=a_raw[0][:], in_=a_rows[:, :, :V])
-        nc.sync.dma_start(pos_sb[0][:], pos1)
         nc.sync.dma_start(pos_sb[1][:], pos2)
         nc.sync.dma_start(out=w3_raw[:], in_=w3.rearrange("(p j) c -> p j c", j=PACK))
         nc.sync.dma_start(out=a_raw[1][:], in_=a_rows[:, :, V:])
+        nc.sync.dma_start(pos_sb[0][:], pos1)
         nc.sync.dma_start(out=w2_codes[:].bitcast(I32), in_=w2_words[0].bitcast(I32))
         for q in range(P // QUADRANT):
             nc.sync.dma_start(
@@ -146,7 +147,7 @@ def tile_picked_dime_none_e_kernel(tc, xT, aT, w1, w3, w2_words, w2_scales, offs
         def pick(t):
             nc.vector.tensor_copy(picked[t // 2][:, t % 2, :], h[t][:].indirect(pos_sb[1][:]))
 
-        w3_grouped = [sb([P, 2, P, PACK], BF16, "w3_grouped%d" % pair) for pair in range(2)]
+        w3_grouped = [sb([P, 2, P, PACK], BF16, "w3_grouped%d" % pair, tag=("w3_grouped0", "w1_codes")[pair]) for pair in range(2)]
         w3_codes = sb([P, H], U32, "w3_codes")
         w3_plane = sb([P, H], U8, "w3_plane")
 
@@ -165,34 +166,39 @@ def tile_picked_dime_none_e_kernel(tc, xT, aT, w1, w3, w2_words, w2_scales, offs
         pick(0)
         pick(1)
         deal_weights(nc.vector.tensor_copy, w3_grouped[0], w3_raw, 0, slice(0, P))
-        deal_weights(nc.vector.tensor_copy, w3_grouped[1], w3_raw, 1, slice(0, P))
+        deal_weights(nc.scalar.copy, w3_grouped[1], w3_raw, 1, slice(0, W3_CUT))
+        deal_weights(nc.vector.tensor_copy, w3_grouped[1], w3_raw, 1, slice(W3_CUT, P))
         quantize_w3(0)
-        filter_pair(0, 0)
+        first_banks = [psum.tile([P, V], F32, name="f_bank0%d" % t, tag="bank%d" % (5 * (1 - t))) for t in range(2)]
+        for t in range(2):
+            hidden_tile(first_banks[t][:], w3_codes, w3_plane, t, a_codes[0][:, :], a_plane[0][:, :])
         quantize_w3(1)
         filter_pair(0, 1)
-        picked.append(sb([P, 2, V], F32, "picked1", tag="w3_raw"))
+        picked.append(sb([P, 1, V], F32, "picked1", tag="w3_grouped0"))
         pick(2)
-        pick(3)
         a_grouped1 = sb([P, V, PACK], BF16, "a_grouped1", tag="w1_plane")
         interleave(nc.scalar.copy, a_grouped1, a_raw[1], slice(0, V))
-        filters = sb([P, PACK, V], F32, "filters")
-        for pair in range(2):
-            nc.scalar.copy(out=filters[:, 2 * pair:2 * pair + 2, :], in_=f_bank[0, pair][:])
+        filters = [sb([P, PACK, V], F32, "filters0"), sb([P, V], F32, "filters1")]
+        for t in range(2):
+            nc.scalar.copy(out=filters[0][:, t, :], in_=first_banks[t][:])
+        nc.scalar.copy(out=filters[0][:, 2:, :], in_=f_bank[0, 1][:])
 
         term = [sb([P, PACK, V], F32, "term%d" % d) for d in range(D)]
 
-        def pick_times_filter(t):
-            nc.vector.tensor_tensor(term[0][:, t, :], h[t][:].indirect(pos_sb[0][:]), filters[:, t, :], MULT)
-
         quantize(nc, a_codes[1][:], a_plane[1][:], a_grouped1[:].rearrange("p v j -> p (v j)"))
+        last_bank = psum.tile([P, V], F32, name="f_bank13", tag="bank1")
+        hidden_tile(last_bank[:], w3_codes, w3_plane, 3, a_codes[1][:, :], a_plane[1][:, :])
+        nc.scalar.copy(out=filters[1][:], in_=last_bank[:])
         filter_pair(1, 0)
-        filter_pair(1, 1)
+        third_bank = psum.tile([P, V], F32, name="f_bank12", tag="bank1")
+        hidden_tile(third_bank[:], w3_codes, w3_plane, 2, a_codes[1][:, :], a_plane[1][:, :])
         for t in range(PACK):
-            pick_times_filter(t)
+            nc.vector.tensor_tensor(term[0][:, t, :], h[t][:].indirect(pos_sb[0][:]), filters[0][:, t, :], MULT)
+        nc.vector.tensor_tensor(term[1][:, 3, :], h[3][:].indirect(pos_sb[1][:]), filters[1][:], MULT)
         target_halves = [slice(u * P, (u + 1) * P) for u in range(V // P)]
         nc.vector.tensor_tensor(term[1][:, 0:2, :], f_bank[1, 0][:], picked[0][:], MULT)
         for targets in target_halves:
-            nc.vector.tensor_tensor(term[1][:, 2:, targets], f_bank[1, 1][:, :, targets], picked[1][:, :, targets], MULT)
+            nc.vector.tensor_tensor(term[1][:, 2, targets], third_bank[:, targets], picked[1][:, 0, targets], MULT)
 
         z_grouped = sb([P, V, PACK], BF16, "z_grouped")
         z_codes = sb([P, V], U32, "z_codes")
@@ -210,7 +216,7 @@ def tile_picked_dime_none_e_kernel(tc, xT, aT, w1, w3, w2_words, w2_scales, offs
         result = [sb([P, V], F32, "result%d" % b) for b in range(N // P)]
         for u, targets in enumerate(target_halves):
             for b, copy in enumerate((nc.scalar.copy, nc.vector.tensor_copy)):
-                bank = psum.tile([P, P], F32, name="out_bank%d%d" % (u, b), tag="bank%d" % (1 + 2 * u + b))
+                bank = psum.tile([P, P], F32, name="out_bank%d%d" % (u, b), tag="bank%d" % (2 + 2 * u + b))
                 nc.tensor.matmul_mx(
                     out=bank[:],
                     lhsT=w2_codes[:, 2 * b * P:2 * (b + 1) * P].bitcast(FP4X4),
@@ -221,5 +227,5 @@ def tile_picked_dime_none_e_kernel(tc, xT, aT, w1, w3, w2_words, w2_scales, offs
                     stop=True,
                 )
                 copy(out=result[b][:, targets], in_=bank[:])
-        nc.scalar.dma_start(out=out[0:P, :], in_=result[0][:])
-        nc.sync.dma_start(out=out[P:N, :], in_=result[1][:])
+                queue = nc.scalar if (u, b) == (1, 0) else nc.sync
+                queue.dma_start(out=out[b * P:(b + 1) * P, targets], in_=result[b][:, targets])

@@ -23,14 +23,14 @@ PACK = 4
 LINE = 4
 LIST_COLUMN = 16
 QUADRANT = 32
-W1_CUTS = (60, 68)
-W3_CUT = 44
+W1_CUT = 32
+W3_CUT = 36
 
 
-def deal_weights(copy, grouped, raw, pair, ms):
+def deal_weights(copy, grouped, raw, pair, ms, first=0):
     copy(
         out=grouped[:].rearrange("p e m j -> p m j e")[:, ms],
-        in_=raw[:].rearrange("p j (m t) -> p m j t", t=PACK)[:, ms, :, 2 * pair:2 * pair + 2],
+        in_=raw[:].rearrange("p j (m t) -> p m j t", t=PACK)[:, ms.start - first:ms.stop - first, :, 2 * pair:2 * pair + 2],
     )
 
 
@@ -56,7 +56,7 @@ def tile_picked_dime_none_e_kernel(tc, xT, aT, w1, w3, w2_words, w2_scales, offs
 
         offs_sb = sb([P, S // LIST_COLUMN], U16, "offs_sb")
         pos_sb = [sb([P, V // LIST_COLUMN], U16, "pos%d_sb" % d) for d in range(D)]
-        w1_raw = sb([P, PACK, H], F32, "w1_raw")
+        w1_raw = [sb([P, PACK, H // 2], F32, "w1_raw%d" % u) for u in range(2)]
         w3_raw = sb([P, PACK, H], F32, "w3_raw")
         x_raw = [sb([P, T], F32, "x_raw%d" % j) for j in range(PACK)]
         a_raw = [sb([P, PACK, V], F32, "a_raw%d" % d) for d in range(D)]
@@ -75,7 +75,9 @@ def tile_picked_dime_none_e_kernel(tc, xT, aT, w1, w3, w2_words, w2_scales, offs
         nc.sync.dma_start(offs_sb[:], offs)
         for j in range(1, PACK):
             nc.sync.dma_start(out=x_raw[j][:], in_=x_rows[:, j, :])
-        nc.sync.dma_start(out=w1_raw[:], in_=w1.rearrange("(p j) c -> p j c", j=PACK))
+        w1_rows = w1.rearrange("(p j) c -> p j c", j=PACK)
+        for u in range(2):
+            nc.sync.dma_start(out=w1_raw[u][:], in_=w1_rows[:, :, u * H // 2:(u + 1) * H // 2])
         nc.sync.dma_start(out=a_raw[0][:], in_=a_rows[:, :, :V])
         nc.sync.dma_start(pos_sb[1][:], pos2)
         nc.sync.dma_start(out=w3_raw[:], in_=w3.rearrange("(p j) c -> p j c", j=PACK))
@@ -105,9 +107,12 @@ def tile_picked_dime_none_e_kernel(tc, xT, aT, w1, w3, w2_words, w2_scales, offs
         w1_grouped = [sb([P, 2, P, PACK], BF16, "w1_grouped%d" % pair) for pair in range(2)]
         w1_codes = sb([P, H], U32, "w1_codes")
         w1_plane = sb([P, H], U8, "w1_plane")
-        for pair, cut in enumerate(W1_CUTS):
-            deal_weights(nc.scalar.copy, w1_grouped[pair], w1_raw, pair, slice(0, cut))
-            deal_weights(nc.vector.tensor_copy, w1_grouped[pair], w1_raw, pair, slice(cut, P))
+        half = P // 2
+        for pair in range(2):
+            deal_weights(nc.scalar.copy, w1_grouped[pair], w1_raw[0], pair, slice(0, half))
+        deal_weights(nc.vector.tensor_copy, w1_grouped[0], w1_raw[1], 0, slice(half, P), half)
+        deal_weights(nc.scalar.copy, w1_grouped[1], w1_raw[1], 1, slice(half, half + W1_CUT), half)
+        deal_weights(nc.vector.tensor_copy, w1_grouped[1], w1_raw[1], 1, slice(half + W1_CUT, P), half)
 
         def hidden_tile(bank, w_codes, w_plane, t, codes, plane):
             nc.tensor.matmul_mx(
@@ -129,12 +134,13 @@ def tile_picked_dime_none_e_kernel(tc, xT, aT, w1, w3, w2_words, w2_scales, offs
         a_grouped0 = sb([P, V, PACK], BF16, "a_grouped0", tag="x_grouped")
         quantize_w1(0, 1)
         quantize_w1(1, 2)
-        interleave(nc.vector.tensor_copy, a_grouped0, a_raw[0], slice(0, V))
         quantize_w1(2, 4)
+        interleave(nc.vector.tensor_copy, a_grouped0, a_raw[0], slice(0, P))
+        interleave(nc.vector.tensor_copy, a_grouped0, a_raw[0], slice(P, V))
 
         h = [sb([P, S], F32, "h%d" % t) for t in range(PACK)]
-        for u, entries in enumerate(entry_halves):
-            bank = psum.tile([P, S // 2], F32, name="h_bank0%d" % u, tag="bank%d" % u)
+        for u, entries in enumerate((slice(0, P), slice(P, 2 * P), slice(2 * P, S))):
+            bank = psum.tile([P, entries.stop - entries.start], F32, name="h_bank0%d" % u, tag="bank%d" % (0, 5, 1)[u])
             hidden_tile(bank[:], w1_codes, w1_plane, 0, x_codes[:, entries], x_plane[:, entries])
             nc.scalar.activation(out=h[0][:, entries], in_=bank[:], func=SILU, bias=zero_bias)
         for t in range(1, PACK):
@@ -142,7 +148,8 @@ def tile_picked_dime_none_e_kernel(tc, xT, aT, w1, w3, w2_words, w2_scales, offs
             hidden_tile(bank[:], w1_codes, w1_plane, t, x_codes[:, :], x_plane[:, :])
             nc.scalar.activation(out=h[t][:], in_=bank[:], func=SILU, bias=zero_bias)
 
-        picked = [sb([P, 2, V], F32, "picked0")]
+        target_halves = [slice(u * P, (u + 1) * P) for u in range(V // P)]
+        picked = [sb([P, 2, V], F32, "picked0", tag="a_raw0")]
 
         def pick(t):
             nc.vector.tensor_copy(picked[t // 2][:, t % 2, :], h[t][:].indirect(pos_sb[1][:]))
@@ -162,7 +169,8 @@ def tile_picked_dime_none_e_kernel(tc, xT, aT, w1, w3, w2_words, w2_scales, offs
             for e in range(2):
                 hidden_tile(f_bank[d, pair][:, e, :], w3_codes, w3_plane, 2 * pair + e, a_codes[d][:, :], a_plane[d][:, :])
 
-        quantize(nc, a_codes[0][:], a_plane[0][:], a_grouped0[:].rearrange("p v j -> p (v j)"))
+        for targets in target_halves:
+            quantize(nc, a_codes[0][:, targets], a_plane[0][:, targets], a_grouped0[:, targets, :].rearrange("p v j -> p (v j)"))
         pick(0)
         pick(1)
         deal_weights(nc.vector.tensor_copy, w3_grouped[0], w3_raw, 0, slice(0, P))
@@ -189,16 +197,17 @@ def tile_picked_dime_none_e_kernel(tc, xT, aT, w1, w3, w2_words, w2_scales, offs
         last_bank = psum.tile([P, V], F32, name="f_bank13", tag="bank1")
         hidden_tile(last_bank[:], w3_codes, w3_plane, 3, a_codes[1][:, :], a_plane[1][:, :])
         nc.scalar.copy(out=filters[1][:], in_=last_bank[:])
-        filter_pair(1, 0)
-        third_bank = psum.tile([P, V], F32, name="f_bank12", tag="bank1")
+        third_bank = psum.tile([P, V], F32, name="f_bank12", tag="bank7")
         hidden_tile(third_bank[:], w3_codes, w3_plane, 2, a_codes[1][:, :], a_plane[1][:, :])
+        f_bank[1, 0] = psum.tile([P, 2, V], F32, name="f_bank10", tag="bank1")
+        for t in range(2):
+            hidden_tile(f_bank[1, 0][:, t, :], w3_codes, w3_plane, t, a_codes[1][:, :], a_plane[1][:, :])
         for t in range(PACK):
             nc.vector.tensor_tensor(term[0][:, t, :], h[t][:].indirect(pos_sb[0][:]), filters[0][:, t, :], MULT)
         nc.vector.tensor_tensor(term[1][:, 3, :], h[3][:].indirect(pos_sb[1][:]), filters[1][:], MULT)
-        target_halves = [slice(u * P, (u + 1) * P) for u in range(V // P)]
-        nc.vector.tensor_tensor(term[1][:, 0:2, :], f_bank[1, 0][:], picked[0][:], MULT)
+        nc.vector.tensor_tensor(term[1][:, 2, :], third_bank[:], picked[1][:, 0, :], MULT)
         for targets in target_halves:
-            nc.vector.tensor_tensor(term[1][:, 2, targets], third_bank[:, targets], picked[1][:, 0, targets], MULT)
+            nc.vector.tensor_tensor(term[1][:, 0:2, targets], f_bank[1, 0][:, :, targets], picked[0][:, :, targets], MULT)
 
         z_grouped = sb([P, V, PACK], BF16, "z_grouped")
         z_codes = sb([P, V], U32, "z_codes")

@@ -24,7 +24,8 @@ LINE = 4
 LIST_COLUMN = 16
 QUADRANT = 32
 W1_CUT = 32
-W3_CUT = 36
+W3_CUT = 80
+A1_CUT = 160
 
 
 def deal_weights(copy, grouped, raw, pair, ms, first=0):
@@ -182,10 +183,11 @@ def tile_picked_dime_none_e_kernel(tc, xT, aT, w1, w3, w2_words, w2_scales, offs
             hidden_tile(first_banks[t][:], w3_codes, w3_plane, t, a_codes[0][:, :], a_plane[0][:, :])
         quantize_w3(1)
         filter_pair(0, 1)
+        a_grouped1 = sb([P, V, PACK], BF16, "a_grouped1", tag="w1_plane")
+        interleave(nc.scalar.copy, a_grouped1, a_raw[1], slice(0, A1_CUT))
+        interleave(nc.vector.tensor_copy, a_grouped1, a_raw[1], slice(A1_CUT, V))
         picked.append(sb([P, 1, V], F32, "picked1", tag="w3_grouped0"))
         pick(2)
-        a_grouped1 = sb([P, V, PACK], BF16, "a_grouped1", tag="w1_plane")
-        interleave(nc.scalar.copy, a_grouped1, a_raw[1], slice(0, V))
         filters = [sb([P, PACK, V], F32, "filters0"), sb([P, V], F32, "filters1")]
         for t in range(2):
             nc.scalar.copy(out=filters[0][:, t, :], in_=first_banks[t][:])
@@ -214,9 +216,9 @@ def tile_picked_dime_none_e_kernel(tc, xT, aT, w1, w3, w2_words, w2_scales, offs
         z_plane = sb([P, V], U8, "z_plane")
         for targets in target_halves:
             nc.vector.tensor_tensor(
-                z_grouped[:, targets, :].rearrange("p (c i) t -> p c t i", i=LINE),
-                term[0][:, :, targets].rearrange("p t (c i) -> p c t i", i=LINE),
-                term[1][:, :, targets].rearrange("p t (c i) -> p c t i", i=LINE),
+                z_grouped[:, targets, :].rearrange("p (c i) t -> p c t i", i=2),
+                term[0][:, :, targets].rearrange("p t (c i) -> p c t i", i=2),
+                term[1][:, :, targets].rearrange("p t (c i) -> p c t i", i=2),
                 ADD,
             )
         for targets in target_halves:

@@ -23,9 +23,9 @@ PACK = 4
 LINE = 4
 LIST_COLUMN = 16
 QUADRANT = 32
-W1_CUT = 32
-W3_CUT = 80
-A1_CUT = 160
+W1_CUT = 80
+W3_CUT = 92
+A1_CUT = 184
 
 
 def deal_weights(copy, grouped, raw, pair, ms, first=0):
@@ -57,7 +57,8 @@ def tile_picked_dime_none_e_kernel(tc, xT, aT, w1, w3, w2_words, w2_scales, offs
 
         offs_sb = sb([P, S // LIST_COLUMN], U16, "offs_sb")
         pos_sb = [sb([P, V // LIST_COLUMN], U16, "pos%d_sb" % d) for d in range(D)]
-        w1_raw = [sb([P, PACK, H // 2], F32, "w1_raw%d" % u) for u in range(2)]
+        w1_parts = [slice(0, W1_CUT), slice(W1_CUT, P)]
+        w1_raw = [sb([P, PACK, PACK * (ms.stop - ms.start)], F32, "w1_raw%d" % u) for u, ms in enumerate(w1_parts)]
         w3_raw = sb([P, PACK, H], F32, "w3_raw")
         x_raw = [sb([P, T], F32, "x_raw%d" % j) for j in range(PACK)]
         a_raw = [sb([P, PACK, V], F32, "a_raw%d" % d) for d in range(D)]
@@ -77,8 +78,8 @@ def tile_picked_dime_none_e_kernel(tc, xT, aT, w1, w3, w2_words, w2_scales, offs
         for j in range(1, PACK):
             nc.sync.dma_start(out=x_raw[j][:], in_=x_rows[:, j, :])
         w1_rows = w1.rearrange("(p j) c -> p j c", j=PACK)
-        for u in range(2):
-            nc.sync.dma_start(out=w1_raw[u][:], in_=w1_rows[:, :, u * H // 2:(u + 1) * H // 2])
+        for u, ms in enumerate(w1_parts):
+            nc.sync.dma_start(out=w1_raw[u][:], in_=w1_rows[:, :, PACK * ms.start:PACK * ms.stop])
         nc.sync.dma_start(out=a_raw[0][:], in_=a_rows[:, :, :V])
         nc.sync.dma_start(pos_sb[1][:], pos2)
         nc.sync.dma_start(out=w3_raw[:], in_=w3.rearrange("(p j) c -> p j c", j=PACK))
@@ -108,12 +109,9 @@ def tile_picked_dime_none_e_kernel(tc, xT, aT, w1, w3, w2_words, w2_scales, offs
         w1_grouped = [sb([P, 2, P, PACK], BF16, "w1_grouped%d" % pair) for pair in range(2)]
         w1_codes = sb([P, H], U32, "w1_codes")
         w1_plane = sb([P, H], U8, "w1_plane")
-        half = P // 2
-        for pair in range(2):
-            deal_weights(nc.scalar.copy, w1_grouped[pair], w1_raw[0], pair, slice(0, half))
-        deal_weights(nc.vector.tensor_copy, w1_grouped[0], w1_raw[1], 0, slice(half, P), half)
-        deal_weights(nc.scalar.copy, w1_grouped[1], w1_raw[1], 1, slice(half, half + W1_CUT), half)
-        deal_weights(nc.vector.tensor_copy, w1_grouped[1], w1_raw[1], 1, slice(half + W1_CUT, P), half)
+        for u, copy in enumerate((nc.scalar.copy, nc.vector.tensor_copy)):
+            for pair in range(2):
+                deal_weights(copy, w1_grouped[pair], w1_raw[u], pair, w1_parts[u], w1_parts[u].start)
 
         def hidden_tile(bank, w_codes, w_plane, t, codes, plane):
             nc.tensor.matmul_mx(
@@ -140,14 +138,12 @@ def tile_picked_dime_none_e_kernel(tc, xT, aT, w1, w3, w2_words, w2_scales, offs
         interleave(nc.vector.tensor_copy, a_grouped0, a_raw[0], slice(P, V))
 
         h = [sb([P, S], F32, "h%d" % t) for t in range(PACK)]
-        for u, entries in enumerate((slice(0, P), slice(P, 2 * P), slice(2 * P, S))):
-            bank = psum.tile([P, entries.stop - entries.start], F32, name="h_bank0%d" % u, tag="bank%d" % (0, 5, 1)[u])
-            hidden_tile(bank[:], w1_codes, w1_plane, 0, x_codes[:, entries], x_plane[:, entries])
-            nc.scalar.activation(out=h[0][:, entries], in_=bank[:], func=SILU, bias=zero_bias)
-        for t in range(1, PACK):
-            bank = psum.tile([P, S], F32, name="h_bank%d" % t, tag="bank%d" % (t + 1))
-            hidden_tile(bank[:], w1_codes, w1_plane, t, x_codes[:, :], x_plane[:, :])
-            nc.scalar.activation(out=h[t][:], in_=bank[:], func=SILU, bias=zero_bias)
+        pieces = [(0, slice(0, P)), (0, slice(P, 2 * P)), (0, entry_halves[1])]
+        pieces = pieces + [(t, entries) for t in range(1, PACK) for entries in entry_halves]
+        for n, (t, entries) in enumerate(pieces):
+            bank = psum.tile([P, entries.stop - entries.start], F32, name="h_bank%d" % n, tag="bank%d" % (n % 8))
+            hidden_tile(bank[:], w1_codes, w1_plane, t, x_codes[:, entries], x_plane[:, entries])
+            nc.scalar.activation(out=h[t][:, entries], in_=bank[:], func=SILU, bias=zero_bias)
 
         target_halves = [slice(u * P, (u + 1) * P) for u in range(V // P)]
         picked = [sb([P, 2, V], F32, "picked0", tag="a_raw0")]
@@ -166,7 +162,7 @@ def tile_picked_dime_none_e_kernel(tc, xT, aT, w1, w3, w2_words, w2_scales, offs
         f_bank = {}
 
         def filter_pair(d, pair):
-            f_bank[d, pair] = psum.tile([P, 2, V], F32, name="f_bank%d%d" % (d, pair), tag="bank%d" % ((5 + 2 * d + pair) % 8))
+            f_bank[d, pair] = psum.tile([P, 2, V], F32, name="f_bank%d%d" % (d, pair), tag="bank3")
             for e in range(2):
                 hidden_tile(f_bank[d, pair][:, e, :], w3_codes, w3_plane, 2 * pair + e, a_codes[d][:, :], a_plane[d][:, :])
 
@@ -178,7 +174,7 @@ def tile_picked_dime_none_e_kernel(tc, xT, aT, w1, w3, w2_words, w2_scales, offs
         deal_weights(nc.scalar.copy, w3_grouped[1], w3_raw, 1, slice(0, W3_CUT))
         deal_weights(nc.vector.tensor_copy, w3_grouped[1], w3_raw, 1, slice(W3_CUT, P))
         quantize_w3(0)
-        first_banks = [psum.tile([P, V], F32, name="f_bank0%d" % t, tag="bank%d" % (5 * (1 - t))) for t in range(2)]
+        first_banks = [psum.tile([P, V], F32, name="f_bank0%d" % t, tag="bank%d" % (1 + t)) for t in range(2)]
         for t in range(2):
             hidden_tile(first_banks[t][:], w3_codes, w3_plane, t, a_codes[0][:, :], a_plane[0][:, :])
         quantize_w3(1)
@@ -196,20 +192,22 @@ def tile_picked_dime_none_e_kernel(tc, xT, aT, w1, w3, w2_words, w2_scales, offs
         term = [sb([P, PACK, V], F32, "term%d" % d) for d in range(D)]
 
         quantize(nc, a_codes[1][:], a_plane[1][:], a_grouped1[:].rearrange("p v j -> p (v j)"))
-        last_bank = psum.tile([P, V], F32, name="f_bank13", tag="bank1")
+        last_bank = psum.tile([P, V], F32, name="f_bank13", tag="bank4")
         hidden_tile(last_bank[:], w3_codes, w3_plane, 3, a_codes[1][:, :], a_plane[1][:, :])
-        nc.scalar.copy(out=filters[1][:], in_=last_bank[:])
-        third_bank = psum.tile([P, V], F32, name="f_bank12", tag="bank7")
+        nc.scalar.copy(out=term[1][:, 2, :], in_=last_bank[:])
+        third_bank = psum.tile([P, V], F32, name="f_bank12", tag="bank5")
         hidden_tile(third_bank[:], w3_codes, w3_plane, 2, a_codes[1][:, :], a_plane[1][:, :])
-        f_bank[1, 0] = psum.tile([P, 2, V], F32, name="f_bank10", tag="bank1")
+        nc.scalar.copy(out=filters[1][:, P:], in_=third_bank[:, P:])
+        f_bank[1, 0] = psum.tile([P, 2, V], F32, name="f_bank10", tag="bank4")
         for t in range(2):
             hidden_tile(f_bank[1, 0][:, t, :], w3_codes, w3_plane, t, a_codes[1][:, :], a_plane[1][:, :])
         for t in range(PACK):
             nc.vector.tensor_tensor(term[0][:, t, :], h[t][:].indirect(pos_sb[0][:]), filters[0][:, t, :], MULT)
-        nc.vector.tensor_tensor(term[1][:, 3, :], h[3][:].indirect(pos_sb[1][:]), filters[1][:], MULT)
-        nc.vector.tensor_tensor(term[1][:, 2, :], third_bank[:], picked[1][:, 0, :], MULT)
-        for targets in target_halves:
-            nc.vector.tensor_tensor(term[1][:, 0:2, targets], f_bank[1, 0][:, :, targets], picked[0][:, :, targets], MULT)
+        nc.vector.tensor_tensor(term[1][:, 3, :], h[3][:].indirect(pos_sb[1][:]), term[1][:, 2, :], MULT)
+        nc.gpsimd.tensor_tensor(term[1][:, 2, P:], filters[1][:, P:], picked[1][:, 0, P:], MULT)
+        nc.vector.tensor_tensor(term[1][:, 0:2, :P], f_bank[1, 0][:, :, :P], picked[0][:, :, :P], MULT)
+        nc.vector.tensor_tensor(term[1][:, 2, :P], third_bank[:, :P], picked[1][:, 0, :P], MULT)
+        nc.vector.tensor_tensor(term[1][:, 0:2, P:], f_bank[1, 0][:, :, P:], picked[0][:, :, P:], MULT)
 
         z_grouped = sb([P, V, PACK], BF16, "z_grouped")
         z_codes = sb([P, V], U32, "z_codes")
@@ -227,7 +225,7 @@ def tile_picked_dime_none_e_kernel(tc, xT, aT, w1, w3, w2_words, w2_scales, offs
         result = [sb([P, V], F32, "result%d" % b) for b in range(N // P)]
         for u, targets in enumerate(target_halves):
             for b, copy in enumerate((nc.scalar.copy, nc.vector.tensor_copy)):
-                bank = psum.tile([P, P], F32, name="out_bank%d%d" % (u, b), tag="bank%d" % (2 + 2 * u + b))
+                bank = psum.tile([P, P], F32, name="out_bank%d%d" % (u, b), tag="bank%d" % ((6 + 2 * u + b) % 8))
                 nc.tensor.matmul_mx(
                     out=bank[:],
                     lhsT=w2_codes[:, 2 * b * P:2 * (b + 1) * P].bitcast(FP4X4),

@@ -15,6 +15,7 @@ U8 = mybir.dt.uint8
 FP8X4 = mybir.dt.float8_e4m3fn_x4
 FP4X4 = mybir.dt.float4_e2m1fn_x4
 SILU = mybir.ActivationFunctionType.Silu
+COPY = mybir.ActivationFunctionType.Copy
 MULT = mybir.AluOpType.mult
 ADD = mybir.AluOpType.add
 
@@ -23,9 +24,7 @@ PACK = 4
 LINE = 4
 LIST_COLUMN = 16
 QUADRANT = 32
-W1_CUT = 80
-W3_CUT = 92
-A1_CUT = 184
+W1_CUTS = (0, 40, 88, 128)
 
 
 def deal_weights(copy, grouped, raw, pair, ms, first=0):
@@ -57,9 +56,10 @@ def tile_picked_dime_none_e_kernel(tc, xT, aT, w1, w3, w2_words, w2_scales, offs
 
         offs_sb = sb([P, S // LIST_COLUMN], U16, "offs_sb")
         pos_sb = [sb([P, V // LIST_COLUMN], U16, "pos%d_sb" % d) for d in range(D)]
-        w1_parts = [slice(0, W1_CUT), slice(W1_CUT, P)]
+        w1_parts = [slice(W1_CUTS[u], W1_CUTS[u + 1]) for u in range(3)]
         w1_raw = [sb([P, PACK, PACK * (ms.stop - ms.start)], F32, "w1_raw%d" % u) for u, ms in enumerate(w1_parts)]
-        w3_raw = sb([P, PACK, H], F32, "w3_raw")
+        w3_parts = [slice(0, P // 2), slice(P // 2, P)]
+        w3_raw = [sb([P, PACK, PACK * (ms.stop - ms.start)], F32, "w3_raw%d" % u) for u, ms in enumerate(w3_parts)]
         x_raw = [sb([P, T], F32, "x_raw%d" % j) for j in range(PACK)]
         a_raw = [sb([P, PACK, V], F32, "a_raw%d" % d) for d in range(D)]
         w2_codes = sb([P, 2 * N], U8, "w2_codes")
@@ -80,11 +80,13 @@ def tile_picked_dime_none_e_kernel(tc, xT, aT, w1, w3, w2_words, w2_scales, offs
         w1_rows = w1.rearrange("(p j) c -> p j c", j=PACK)
         for u, ms in enumerate(w1_parts):
             nc.sync.dma_start(out=w1_raw[u][:], in_=w1_rows[:, :, PACK * ms.start:PACK * ms.stop])
-        nc.sync.dma_start(out=a_raw[0][:], in_=a_rows[:, :, :V])
-        nc.sync.dma_start(pos_sb[1][:], pos2)
-        nc.sync.dma_start(out=w3_raw[:], in_=w3.rearrange("(p j) c -> p j c", j=PACK))
-        nc.sync.dma_start(out=a_raw[1][:], in_=a_rows[:, :, V:])
+        w3_rows = w3.rearrange("(p j) c -> p j c", j=PACK)
+        nc.sync.dma_start(out=w3_raw[0][:], in_=w3_rows[:, :, :H // 2])
         nc.sync.dma_start(pos_sb[0][:], pos1)
+        nc.sync.dma_start(out=w3_raw[1][:], in_=w3_rows[:, :, H // 2:])
+        nc.sync.dma_start(pos_sb[1][:], pos2)
+        for d in range(D):
+            nc.sync.dma_start(out=a_raw[d][:], in_=a_rows[:, :, d * V:(d + 1) * V])
         nc.sync.dma_start(out=w2_codes[:].bitcast(I32), in_=w2_words[0].bitcast(I32))
         for q in range(P // QUADRANT):
             nc.sync.dma_start(
@@ -109,7 +111,7 @@ def tile_picked_dime_none_e_kernel(tc, xT, aT, w1, w3, w2_words, w2_scales, offs
         w1_grouped = [sb([P, 2, P, PACK], BF16, "w1_grouped%d" % pair) for pair in range(2)]
         w1_codes = sb([P, H], U32, "w1_codes")
         w1_plane = sb([P, H], U8, "w1_plane")
-        for u, copy in enumerate((nc.scalar.copy, nc.vector.tensor_copy)):
+        for u, copy in enumerate((nc.scalar.copy, nc.scalar.copy, nc.vector.tensor_copy)):
             for pair in range(2):
                 deal_weights(copy, w1_grouped[pair], w1_raw[u], pair, w1_parts[u], w1_parts[u].start)
 
@@ -128,86 +130,60 @@ def tile_picked_dime_none_e_kernel(tc, xT, aT, w1, w3, w2_words, w2_scales, offs
             columns = slice(t0 * P, t1 * P)
             quantize(nc, w1_codes[:, columns], w1_plane[:, columns], w1_grouped[t0 // 2][:, t0 % 2:(t1 - 1) % 2 + 1].rearrange("p e m j -> p (e m j)"))
 
-        a_codes = [sb([P, V], U32, "a_codes%d" % d) for d in range(D)]
-        a_plane = [sb([P, V], U8, "a_plane%d" % d) for d in range(D)]
-        a_grouped0 = sb([P, V, PACK], BF16, "a_grouped0", tag="x_grouped")
         quantize_w1(0, 1)
         quantize_w1(1, 2)
         quantize_w1(2, 4)
-        interleave(nc.vector.tensor_copy, a_grouped0, a_raw[0], slice(0, P))
-        interleave(nc.vector.tensor_copy, a_grouped0, a_raw[0], slice(P, V))
 
         h = [sb([P, S], F32, "h%d" % t) for t in range(PACK)]
         pieces = [(0, slice(0, P)), (0, slice(P, 2 * P)), (0, entry_halves[1])]
         pieces = pieces + [(t, entries) for t in range(1, PACK) for entries in entry_halves]
         for n, (t, entries) in enumerate(pieces):
-            bank = psum.tile([P, entries.stop - entries.start], F32, name="h_bank%d" % n, tag="bank%d" % (n % 8))
+            bank = psum.tile([P, entries.stop - entries.start], F32, name="h_bank%d" % n, tag="bank%d" % (n % 4))
             hidden_tile(bank[:], w1_codes, w1_plane, t, x_codes[:, entries], x_plane[:, entries])
             nc.scalar.activation(out=h[t][:, entries], in_=bank[:], func=SILU, bias=zero_bias)
 
-        target_halves = [slice(u * P, (u + 1) * P) for u in range(V // P)]
-        picked = [sb([P, 2, V], F32, "picked0", tag="a_raw0")]
+        picked = [[sb([P, 2, V], F32, "picked%d%d" % (d, pair)) for pair in range(2)] for d in range(D)]
+        for d in range(D):
+            for t in range(PACK):
+                if (d, t) != (1, 0):
+                    nc.scalar.activation(out=picked[d][t // 2][:, t % 2, :], in_=h[t][:].indirect(pos_sb[d][:]), func=COPY)
 
-        def pick(t):
-            nc.vector.tensor_copy(picked[t // 2][:, t % 2, :], h[t][:].indirect(pos_sb[1][:]))
-
-        w3_grouped = [sb([P, 2, P, PACK], BF16, "w3_grouped%d" % pair, tag=("w3_grouped0", "w1_codes")[pair]) for pair in range(2)]
+        w3_grouped = [sb([P, 2, P, PACK], BF16, "w3_grouped%d" % pair) for pair in range(2)]
         w3_codes = sb([P, H], U32, "w3_codes")
         w3_plane = sb([P, H], U8, "w3_plane")
-
-        def quantize_w3(pair):
+        for u in range(2):
+            for pair in range(2):
+                deal_weights(nc.vector.tensor_copy, w3_grouped[pair], w3_raw[u], pair, w3_parts[u], w3_parts[u].start)
+        for pair in range(2):
             columns = slice(2 * pair * P, 2 * (pair + 1) * P)
             quantize(nc, w3_codes[:, columns], w3_plane[:, columns], w3_grouped[pair][:].rearrange("p e m j -> p (e m j)"))
 
+        target_halves = [slice(u * P, (u + 1) * P) for u in range(V // P)]
         f_bank = {}
-
-        def filter_pair(d, pair):
-            f_bank[d, pair] = psum.tile([P, 2, V], F32, name="f_bank%d%d" % (d, pair), tag="bank3")
-            for e in range(2):
-                hidden_tile(f_bank[d, pair][:, e, :], w3_codes, w3_plane, 2 * pair + e, a_codes[d][:, :], a_plane[d][:, :])
-
-        for targets in target_halves:
-            quantize(nc, a_codes[0][:, targets], a_plane[0][:, targets], a_grouped0[:, targets, :].rearrange("p v j -> p (v j)"))
-        pick(0)
-        pick(1)
-        deal_weights(nc.vector.tensor_copy, w3_grouped[0], w3_raw, 0, slice(0, P))
-        deal_weights(nc.scalar.copy, w3_grouped[1], w3_raw, 1, slice(0, W3_CUT))
-        deal_weights(nc.vector.tensor_copy, w3_grouped[1], w3_raw, 1, slice(W3_CUT, P))
-        quantize_w3(0)
-        first_banks = [psum.tile([P, V], F32, name="f_bank0%d" % t, tag="bank%d" % (1 + t)) for t in range(2)]
-        for t in range(2):
-            hidden_tile(first_banks[t][:], w3_codes, w3_plane, t, a_codes[0][:, :], a_plane[0][:, :])
-        quantize_w3(1)
-        filter_pair(0, 1)
-        a_grouped1 = sb([P, V, PACK], BF16, "a_grouped1", tag="w1_plane")
-        interleave(nc.scalar.copy, a_grouped1, a_raw[1], slice(0, A1_CUT))
-        interleave(nc.vector.tensor_copy, a_grouped1, a_raw[1], slice(A1_CUT, V))
-        picked.append(sb([P, 1, V], F32, "picked1", tag="w3_grouped0"))
-        pick(2)
-        filters = [sb([P, PACK, V], F32, "filters0"), sb([P, V], F32, "filters1")]
-        for t in range(2):
-            nc.scalar.copy(out=filters[0][:, t, :], in_=first_banks[t][:])
-        nc.scalar.copy(out=filters[0][:, 2:, :], in_=f_bank[0, 1][:])
+        for d in range(D):
+            a_grouped = sb([P, V, PACK], BF16, "a_grouped%d" % d)
+            a_codes = sb([P, V], U32, "a_codes%d" % d)
+            a_plane = sb([P, V], U8, "a_plane%d" % d)
+            if d == 0:
+                for targets in target_halves:
+                    interleave(nc.vector.tensor_copy, a_grouped, a_raw[d], targets)
+                for targets in target_halves:
+                    quantize(nc, a_codes[:, targets], a_plane[:, targets], a_grouped[:, targets, :].rearrange("p v j -> p (v j)"))
+            else:
+                interleave(nc.vector.tensor_copy, a_grouped, a_raw[d], slice(0, V))
+                nc.vector.tensor_copy(picked[1][0][:, 0, :], h[0][:].indirect(pos_sb[1][:]))
+                quantize(nc, a_codes[:], a_plane[:], a_grouped[:].rearrange("p v j -> p (v j)"))
+            for pair in range(2):
+                f_bank[d, pair] = psum.tile([P, 2, V], F32, name="f_bank%d%d" % (d, pair), tag="bank%d" % (4 + 2 * d + pair))
+                for e in range(2):
+                    hidden_tile(f_bank[d, pair][:, e, :], w3_codes, w3_plane, 2 * pair + e, a_codes[:, :], a_plane[:, :])
 
         term = [sb([P, PACK, V], F32, "term%d" % d) for d in range(D)]
-
-        quantize(nc, a_codes[1][:], a_plane[1][:], a_grouped1[:].rearrange("p v j -> p (v j)"))
-        last_bank = psum.tile([P, V], F32, name="f_bank13", tag="bank4")
-        hidden_tile(last_bank[:], w3_codes, w3_plane, 3, a_codes[1][:, :], a_plane[1][:, :])
-        nc.scalar.copy(out=term[1][:, 2, :], in_=last_bank[:])
-        third_bank = psum.tile([P, V], F32, name="f_bank12", tag="bank5")
-        hidden_tile(third_bank[:], w3_codes, w3_plane, 2, a_codes[1][:, :], a_plane[1][:, :])
-        nc.scalar.copy(out=filters[1][:, P:], in_=third_bank[:, P:])
-        f_bank[1, 0] = psum.tile([P, 2, V], F32, name="f_bank10", tag="bank4")
-        for t in range(2):
-            hidden_tile(f_bank[1, 0][:, t, :], w3_codes, w3_plane, t, a_codes[1][:, :], a_plane[1][:, :])
-        for t in range(PACK):
-            nc.vector.tensor_tensor(term[0][:, t, :], h[t][:].indirect(pos_sb[0][:]), filters[0][:, t, :], MULT)
-        nc.vector.tensor_tensor(term[1][:, 3, :], h[3][:].indirect(pos_sb[1][:]), term[1][:, 2, :], MULT)
-        nc.gpsimd.tensor_tensor(term[1][:, 2, P:], filters[1][:, P:], picked[1][:, 0, P:], MULT)
-        nc.vector.tensor_tensor(term[1][:, 0:2, :P], f_bank[1, 0][:, :, :P], picked[0][:, :, :P], MULT)
-        nc.vector.tensor_tensor(term[1][:, 2, :P], third_bank[:, :P], picked[1][:, 0, :P], MULT)
-        nc.vector.tensor_tensor(term[1][:, 0:2, P:], f_bank[1, 0][:, :, P:], picked[0][:, :, P:], MULT)
+        for pair in range(2):
+            nc.vector.tensor_tensor(term[0][:, 2 * pair:2 * pair + 2, :], f_bank[0, pair][:], picked[0][pair][:], MULT)
+        for targets in target_halves:
+            for pair in range(2):
+                nc.vector.tensor_tensor(term[1][:, 2 * pair:2 * pair + 2, targets], f_bank[1, pair][:, :, targets], picked[1][pair][:, :, targets], MULT)
 
         z_grouped = sb([P, V, PACK], BF16, "z_grouped")
         z_codes = sb([P, V], U32, "z_codes")
@@ -225,7 +201,7 @@ def tile_picked_dime_none_e_kernel(tc, xT, aT, w1, w3, w2_words, w2_scales, offs
         result = [sb([P, V], F32, "result%d" % b) for b in range(N // P)]
         for u, targets in enumerate(target_halves):
             for b, copy in enumerate((nc.scalar.copy, nc.vector.tensor_copy)):
-                bank = psum.tile([P, P], F32, name="out_bank%d%d" % (u, b), tag="bank%d" % ((6 + 2 * u + b) % 8))
+                bank = psum.tile([P, P], F32, name="out_bank%d%d" % (u, b), tag="bank%d" % (2 * u + b))
                 nc.tensor.matmul_mx(
                     out=bank[:],
                     lhsT=w2_codes[:, 2 * b * P:2 * (b + 1) * P].bitcast(FP4X4),

@@ -24,7 +24,8 @@ PACK = 4
 LINE = 4
 LIST_COLUMN = 16
 QUADRANT = 32
-W1_CUTS = (0, 40, 88, 128)
+W1_CUTS = (0, 48, 96, 128)
+W3_CUT = 64
 
 
 def deal_weights(copy, grouped, raw, pair, ms, first=0):
@@ -58,7 +59,7 @@ def tile_picked_dime_none_e_kernel(tc, xT, aT, w1, w3, w2_words, w2_scales, offs
         pos_sb = [sb([P, V // LIST_COLUMN], U16, "pos%d_sb" % d) for d in range(D)]
         w1_parts = [slice(W1_CUTS[u], W1_CUTS[u + 1]) for u in range(3)]
         w1_raw = [sb([P, PACK, PACK * (ms.stop - ms.start)], F32, "w1_raw%d" % u) for u, ms in enumerate(w1_parts)]
-        w3_parts = [slice(0, P // 2), slice(P // 2, P)]
+        w3_parts = [slice(0, W3_CUT), slice(W3_CUT, P)]
         w3_raw = [sb([P, PACK, PACK * (ms.stop - ms.start)], F32, "w3_raw%d" % u) for u, ms in enumerate(w3_parts)]
         x_raw = [sb([P, T], F32, "x_raw%d" % j) for j in range(PACK)]
         a_raw = [sb([P, PACK, V], F32, "a_raw%d" % d) for d in range(D)]
@@ -81,12 +82,12 @@ def tile_picked_dime_none_e_kernel(tc, xT, aT, w1, w3, w2_words, w2_scales, offs
         for u, ms in enumerate(w1_parts):
             nc.sync.dma_start(out=w1_raw[u][:], in_=w1_rows[:, :, PACK * ms.start:PACK * ms.stop])
         w3_rows = w3.rearrange("(p j) c -> p j c", j=PACK)
-        nc.sync.dma_start(out=w3_raw[0][:], in_=w3_rows[:, :, :H // 2])
         nc.sync.dma_start(pos_sb[0][:], pos1)
-        nc.sync.dma_start(out=w3_raw[1][:], in_=w3_rows[:, :, H // 2:])
+        nc.sync.dma_start(out=a_raw[0][:], in_=a_rows[:, :, :V])
+        nc.sync.dma_start(out=w3_raw[0][:], in_=w3_rows[:, :, :PACK * W3_CUT])
         nc.sync.dma_start(pos_sb[1][:], pos2)
-        for d in range(D):
-            nc.sync.dma_start(out=a_raw[d][:], in_=a_rows[:, :, d * V:(d + 1) * V])
+        nc.sync.dma_start(out=w3_raw[1][:], in_=w3_rows[:, :, PACK * W3_CUT:])
+        nc.sync.dma_start(out=a_raw[1][:], in_=a_rows[:, :, V:])
         nc.sync.dma_start(out=w2_codes[:].bitcast(I32), in_=w2_words[0].bitcast(I32))
         for q in range(P // QUADRANT):
             nc.sync.dma_start(
@@ -134,65 +135,89 @@ def tile_picked_dime_none_e_kernel(tc, xT, aT, w1, w3, w2_words, w2_scales, offs
         quantize_w1(1, 2)
         quantize_w1(2, 4)
 
+        target_halves = [slice(u * P, (u + 1) * P) for u in range(V // P)]
+        a_grouped = [sb([P, V, PACK], BF16, "a_grouped0")]
+        a_codes = [sb([P, V], U32, "a_codes%d" % d) for d in range(D)]
+        a_plane = [sb([P, V], U8, "a_plane%d" % d) for d in range(D)]
+        for targets in target_halves:
+            interleave(nc.vector.tensor_copy, a_grouped[0], a_raw[0], targets)
+        for targets in target_halves:
+            quantize(nc, a_codes[0][:, targets], a_plane[0][:, targets], a_grouped[0][:, targets, :].rearrange("p v j -> p (v j)"))
+
         h = [sb([P, S], F32, "h%d" % t) for t in range(PACK)]
-        pieces = [(0, slice(0, P)), (0, slice(P, 2 * P)), (0, entry_halves[1])]
-        pieces = pieces + [(t, entries) for t in range(1, PACK) for entries in entry_halves]
+        picked = [[sb([P, 2, V], F32, "picked%d%d" % (d, pair)) for pair in range(2)] for d in range(D)]
+
+        def window(d, t, targets):
+            return h[t][:].indirect(pos_sb[d][:, targets.start // LIST_COLUMN:targets.stop // LIST_COLUMN])
+
+        def pick(d, t, targets):
+            nc.scalar.activation(out=picked[d][t // 2][:, t % 2, targets], in_=window(d, t, targets), func=COPY)
+
+        pieces = [(0, slice(0, P)), (0, slice(P, 2 * P)), (0, entry_halves[1])] + [(t, slice(0, S)) for t in range(1, PACK)]
         for n, (t, entries) in enumerate(pieces):
             bank = psum.tile([P, entries.stop - entries.start], F32, name="h_bank%d" % n, tag="bank%d" % (n % 4))
             hidden_tile(bank[:], w1_codes, w1_plane, t, x_codes[:, entries], x_plane[:, entries])
             nc.scalar.activation(out=h[t][:, entries], in_=bank[:], func=SILU, bias=zero_bias)
-
-        picked = [[sb([P, 2, V], F32, "picked%d%d" % (d, pair)) for pair in range(2)] for d in range(D)]
-        for d in range(D):
-            for t in range(PACK):
-                if (d, t) != (1, 0):
-                    nc.scalar.activation(out=picked[d][t // 2][:, t % 2, :], in_=h[t][:].indirect(pos_sb[d][:]), func=COPY)
+        first, second = target_halves
+        whole = slice(0, V)
+        for t in range(PACK):
+            pick(0, t, whole)
+        pick(1, 1, second)
+        for t in range(2, PACK):
+            pick(1, t, whole)
 
         w3_grouped = [sb([P, 2, P, PACK], BF16, "w3_grouped%d" % pair) for pair in range(2)]
         w3_codes = sb([P, H], U32, "w3_codes")
         w3_plane = sb([P, H], U8, "w3_plane")
-        for u in range(2):
-            for pair in range(2):
-                deal_weights(nc.vector.tensor_copy, w3_grouped[pair], w3_raw[u], pair, w3_parts[u], w3_parts[u].start)
+        for pair in range(2):
+            deal_weights(nc.vector.tensor_copy, w3_grouped[pair], w3_raw[0], pair, w3_parts[0], 0)
+        nc.vector.tensor_copy(picked[1][0][:, 0, :], window(1, 0, whole))
+        nc.vector.tensor_copy(picked[1][0][:, 1, first], window(1, 1, first))
+        for pair in range(2):
+            deal_weights(nc.vector.tensor_copy, w3_grouped[pair], w3_raw[1], pair, w3_parts[1], W3_CUT)
+        f_bank = {}
+
+        def filters(d, pair):
+            f_bank[d, pair] = psum.tile([P, 2, V], F32, name="f_bank%d%d" % (d, pair), tag="bank%d" % (4 + 2 * d + pair))
+            for e in range(2):
+                hidden_tile(f_bank[d, pair][:, e, :], w3_codes, w3_plane, 2 * pair + e, a_codes[d][:, :], a_plane[d][:, :])
+
         for pair in range(2):
             columns = slice(2 * pair * P, 2 * (pair + 1) * P)
             quantize(nc, w3_codes[:, columns], w3_plane[:, columns], w3_grouped[pair][:].rearrange("p e m j -> p (e m j)"))
+            filters(0, pair)
 
-        target_halves = [slice(u * P, (u + 1) * P) for u in range(V // P)]
-        f_bank = {}
-        for d in range(D):
-            a_grouped = sb([P, V, PACK], BF16, "a_grouped%d" % d)
-            a_codes = sb([P, V], U32, "a_codes%d" % d)
-            a_plane = sb([P, V], U8, "a_plane%d" % d)
-            if d == 0:
-                for targets in target_halves:
-                    interleave(nc.vector.tensor_copy, a_grouped, a_raw[d], targets)
-                for targets in target_halves:
-                    quantize(nc, a_codes[:, targets], a_plane[:, targets], a_grouped[:, targets, :].rearrange("p v j -> p (v j)"))
-            else:
-                interleave(nc.vector.tensor_copy, a_grouped, a_raw[d], slice(0, V))
-                nc.vector.tensor_copy(picked[1][0][:, 0, :], h[0][:].indirect(pos_sb[1][:]))
-                quantize(nc, a_codes[:], a_plane[:], a_grouped[:].rearrange("p v j -> p (v j)"))
-            for pair in range(2):
-                f_bank[d, pair] = psum.tile([P, 2, V], F32, name="f_bank%d%d" % (d, pair), tag="bank%d" % (4 + 2 * d + pair))
-                for e in range(2):
-                    hidden_tile(f_bank[d, pair][:, e, :], w3_codes, w3_plane, 2 * pair + e, a_codes[:, :], a_plane[:, :])
+        term = [sb([P, V // P, PACK, P], F32, "term%d" % d) for d in range(D)]
 
-        term = [sb([P, PACK, V], F32, "term%d" % d) for d in range(D)]
-        for pair in range(2):
-            nc.vector.tensor_tensor(term[0][:, 2 * pair:2 * pair + 2, :], f_bank[0, pair][:], picked[0][pair][:], MULT)
+        def product(d, pair, targets):
+            nc.vector.tensor_tensor(
+                term[d][:, targets.start // P:targets.stop // P, 2 * pair:2 * pair + 2, :].rearrange("p u e v -> p e u v"),
+                f_bank[d, pair][:, :, targets].rearrange("p e (u v) -> p e u v", v=P),
+                picked[d][pair][:, :, targets].rearrange("p e (u v) -> p e u v", v=P),
+                MULT,
+            )
+
+        a_grouped.append(sb([P, V, PACK], BF16, "a_grouped1", tag="w3_grouped0"))
         for targets in target_halves:
-            for pair in range(2):
-                nc.vector.tensor_tensor(term[1][:, 2 * pair:2 * pair + 2, targets], f_bank[1, pair][:, :, targets], picked[1][pair][:, :, targets], MULT)
+            interleave(nc.vector.tensor_copy, a_grouped[1], a_raw[1], targets)
+        for targets in target_halves:
+            quantize(nc, a_codes[1][:, targets], a_plane[1][:, targets], a_grouped[1][:, targets, :].rearrange("p v j -> p (v j)"))
+        for pair in range(2):
+            filters(1, pair)
+        product(0, 0, slice(0, V))
+        product(0, 1, slice(0, V))
+        product(1, 0, slice(0, V))
+        for targets in target_halves:
+            product(1, 1, targets)
 
         z_grouped = sb([P, V, PACK], BF16, "z_grouped")
         z_codes = sb([P, V], U32, "z_codes")
         z_plane = sb([P, V], U8, "z_plane")
-        for targets in target_halves:
+        for u, targets in enumerate(target_halves):
             nc.vector.tensor_tensor(
                 z_grouped[:, targets, :].rearrange("p (c i) t -> p c t i", i=2),
-                term[0][:, :, targets].rearrange("p t (c i) -> p c t i", i=2),
-                term[1][:, :, targets].rearrange("p t (c i) -> p c t i", i=2),
+                term[0][:, u].rearrange("p t (c i) -> p c t i", i=2),
+                term[1][:, u].rearrange("p t (c i) -> p c t i", i=2),
                 ADD,
             )
         for targets in target_halves:

@@ -24,8 +24,7 @@ PACK = 4
 LINE = 4
 LIST_COLUMN = 16
 QUADRANT = 32
-W1_CUTS = (0, 48, 96, 128)
-W3_CUT = 64
+W1_CUTS = (0, 64, 96, 128)
 
 
 def deal_weights(copy, grouped, raw, pair, ms, first=0):
@@ -46,6 +45,10 @@ def quantize(nc, codes, plane, grouped):
     nc.vector.quantize_mx(out=codes.bitcast(FP8X4), scales=plane, in_=grouped)
 
 
+def list_columns(entries):
+    return slice(entries.start // LIST_COLUMN, entries.stop // LIST_COLUMN)
+
+
 def tile_picked_dime_none_e_kernel(tc, xT, aT, w1, w3, w2_words, w2_scales, offs, pos1, pos2, out):
     nc = tc.nc
     with ExitStack() as ctx:
@@ -53,14 +56,14 @@ def tile_picked_dime_none_e_kernel(tc, xT, aT, w1, w3, w2_words, w2_scales, offs
         psum = ctx.enter_context(tc.psum_pool(name="psum", bufs=1))
 
         def sb(shape, dtype, name, tag=None):
-            return keep.tile(shape, dtype, name=name, tag=tag or name, align_bytes=64)
+            return keep.tile(shape, dtype, name=name, tag=tag or name, align_bytes=256)
 
         offs_sb = sb([P, S // LIST_COLUMN], U16, "offs_sb")
         pos_sb = [sb([P, V // LIST_COLUMN], U16, "pos%d_sb" % d) for d in range(D)]
         w1_parts = [slice(W1_CUTS[u], W1_CUTS[u + 1]) for u in range(3)]
         w1_raw = [sb([P, PACK, PACK * (ms.stop - ms.start)], F32, "w1_raw%d" % u) for u, ms in enumerate(w1_parts)]
-        w3_parts = [slice(0, W3_CUT), slice(W3_CUT, P)]
-        w3_raw = [sb([P, PACK, PACK * (ms.stop - ms.start)], F32, "w3_raw%d" % u) for u, ms in enumerate(w3_parts)]
+        w3_parts = [slice(0, P // 2), slice(P // 2, P)]
+        w3_raw = [sb([P, PACK, H // 2], F32, "w3_raw%d" % u) for u in range(2)]
         x_raw = [sb([P, T], F32, "x_raw%d" % j) for j in range(PACK)]
         a_raw = [sb([P, PACK, V], F32, "a_raw%d" % d) for d in range(D)]
         w2_codes = sb([P, 2 * N], U8, "w2_codes")
@@ -74,19 +77,19 @@ def tile_picked_dime_none_e_kernel(tc, xT, aT, w1, w3, w2_words, w2_scales, offs
 
         x_rows = xT.rearrange("(p j) t -> p j t", j=PACK)
         a_rows = aT.rearrange("(p j) u -> p j u", j=PACK)
+        w3_rows = w3.rearrange("(p j) c -> p j c", j=PACK)
+        w1_rows = w1.rearrange("(p j) c -> p j c", j=PACK)
         nc.sync.dma_start(out=x_raw[0][:], in_=x_rows[:, 0, :])
         nc.sync.dma_start(offs_sb[:], offs)
         for j in range(1, PACK):
             nc.sync.dma_start(out=x_raw[j][:], in_=x_rows[:, j, :])
-        w1_rows = w1.rearrange("(p j) c -> p j c", j=PACK)
         for u, ms in enumerate(w1_parts):
             nc.sync.dma_start(out=w1_raw[u][:], in_=w1_rows[:, :, PACK * ms.start:PACK * ms.stop])
-        w3_rows = w3.rearrange("(p j) c -> p j c", j=PACK)
         nc.sync.dma_start(pos_sb[0][:], pos1)
         nc.sync.dma_start(out=a_raw[0][:], in_=a_rows[:, :, :V])
-        nc.sync.dma_start(out=w3_raw[0][:], in_=w3_rows[:, :, :PACK * W3_CUT])
+        nc.sync.dma_start(out=w3_raw[0][:], in_=w3_rows[:, :, :H // 2])
         nc.sync.dma_start(pos_sb[1][:], pos2)
-        nc.sync.dma_start(out=w3_raw[1][:], in_=w3_rows[:, :, PACK * W3_CUT:])
+        nc.sync.dma_start(out=w3_raw[1][:], in_=w3_rows[:, :, H // 2:])
         nc.sync.dma_start(out=a_raw[1][:], in_=a_rows[:, :, V:])
         nc.sync.dma_start(out=w2_codes[:].bitcast(I32), in_=w2_words[0].bitcast(I32))
         for q in range(P // QUADRANT):
@@ -95,26 +98,25 @@ def tile_picked_dime_none_e_kernel(tc, xT, aT, w1, w3, w2_words, w2_scales, offs
                 in_=w2_scales[0, 4 * q:4 * q + 4, :].bitcast(I32),
             )
 
-        x_grouped = sb([P, S, PACK], BF16, "x_grouped")
-        entry_halves = [slice(u * S // 2, (u + 1) * S // 2) for u in range(2)]
-        for j in range(PACK - 1):
-            nc.vector.tensor_copy(x_grouped[:, :, j], x_raw[j][:].indirect(offs_sb[:]))
-        for entries in entry_halves:
-            nc.vector.tensor_copy(
-                x_grouped[:, entries, PACK - 1],
-                x_raw[PACK - 1][:].indirect(offs_sb[:, entries.start // LIST_COLUMN:entries.stop // LIST_COLUMN]),
-            )
+        halves = [slice(u * S // 2, (u + 1) * S // 2) for u in range(2)]
+        x_grouped = [sb([P, S // 2, PACK], BF16, "x_grouped%d" % u) for u in range(2)]
+        for j in range(PACK):
+            nc.vector.tensor_copy(x_grouped[0][:, :, j], x_raw[j][:].indirect(offs_sb[:, list_columns(halves[0])]))
+            nc.scalar.activation(out=x_grouped[1][:, :, j], in_=x_raw[j][:].indirect(offs_sb[:, list_columns(halves[1])]), func=COPY)
         x_plane = sb([P, S], U8, "x_plane")
         x_codes = sb([P, S], U32, "x_codes")
-        for entries in entry_halves:
-            quantize(nc, x_codes[:, entries], x_plane[:, entries], x_grouped[:, entries, :].rearrange("p s j -> p (s j)"))
+        for u in range(2):
+            quantize(nc, x_codes[:, halves[u]], x_plane[:, halves[u]], x_grouped[u][:].rearrange("p s j -> p (s j)"))
 
         w1_grouped = [sb([P, 2, P, PACK], BF16, "w1_grouped%d" % pair) for pair in range(2)]
         w1_codes = sb([P, H], U32, "w1_codes")
         w1_plane = sb([P, H], U8, "w1_plane")
-        for u, copy in enumerate((nc.scalar.copy, nc.scalar.copy, nc.vector.tensor_copy)):
-            for pair in range(2):
+        for u in range(3):
+            for pair, copy in enumerate((nc.vector.tensor_copy, nc.scalar.copy if u < 2 else nc.vector.tensor_copy)):
                 deal_weights(copy, w1_grouped[pair], w1_raw[u], pair, w1_parts[u], w1_parts[u].start)
+        for t0, t1 in ((0, 1), (1, 2), (2, 4)):
+            columns = slice(t0 * P, t1 * P)
+            quantize(nc, w1_codes[:, columns], w1_plane[:, columns], w1_grouped[t0 // 2][:, t0 % 2:(t1 - 1) % 2 + 1].rearrange("p e m j -> p (e m j)"))
 
         def hidden_tile(bank, w_codes, w_plane, t, codes, plane):
             nc.tensor.matmul_mx(
@@ -127,44 +129,41 @@ def tile_picked_dime_none_e_kernel(tc, xT, aT, w1, w3, w2_words, w2_scales, offs
                 stop=True,
             )
 
-        def quantize_w1(t0, t1):
-            columns = slice(t0 * P, t1 * P)
-            quantize(nc, w1_codes[:, columns], w1_plane[:, columns], w1_grouped[t0 // 2][:, t0 % 2:(t1 - 1) % 2 + 1].rearrange("p e m j -> p (e m j)"))
-
-        quantize_w1(0, 1)
-        quantize_w1(1, 2)
-        quantize_w1(2, 4)
-
-        target_halves = [slice(u * P, (u + 1) * P) for u in range(V // P)]
-        a_grouped = [sb([P, V, PACK], BF16, "a_grouped0")]
+        first, second = [slice(u * P, (u + 1) * P) for u in range(V // P)]
+        whole = slice(0, V)
         a_codes = [sb([P, V], U32, "a_codes%d" % d) for d in range(D)]
         a_plane = [sb([P, V], U8, "a_plane%d" % d) for d in range(D)]
-        for targets in target_halves:
-            interleave(nc.vector.tensor_copy, a_grouped[0], a_raw[0], targets)
-        for targets in target_halves:
-            quantize(nc, a_codes[0][:, targets], a_plane[0][:, targets], a_grouped[0][:, targets, :].rearrange("p v j -> p (v j)"))
+
+        def prepare_features(d, tag):
+            grouped = sb([P, V, PACK], BF16, "a_grouped%d" % d, tag=tag)
+            for targets in (first, second):
+                interleave(nc.vector.tensor_copy, grouped, a_raw[d], targets)
+            for targets in (first, second):
+                quantize(nc, a_codes[d][:, targets], a_plane[d][:, targets], grouped[:, targets, :].rearrange("p v j -> p (v j)"))
+
+        prepare_features(0, "a_grouped0")
 
         h = [sb([P, S], F32, "h%d" % t) for t in range(PACK)]
-        picked = [[sb([P, 2, V], F32, "picked%d%d" % (d, pair)) for pair in range(2)] for d in range(D)]
-
-        def window(d, t, targets):
-            return h[t][:].indirect(pos_sb[d][:, targets.start // LIST_COLUMN:targets.stop // LIST_COLUMN])
-
-        def pick(d, t, targets):
-            nc.scalar.activation(out=picked[d][t // 2][:, t % 2, targets], in_=window(d, t, targets), func=COPY)
-
-        pieces = [(0, slice(0, P)), (0, slice(P, 2 * P)), (0, entry_halves[1])] + [(t, slice(0, S)) for t in range(1, PACK)]
+        pieces = [(0, slice(0, P)), (0, slice(P, 2 * P)), (0, halves[1])] + [(t, slice(0, S)) for t in range(1, PACK)]
         for n, (t, entries) in enumerate(pieces):
             bank = psum.tile([P, entries.stop - entries.start], F32, name="h_bank%d" % n, tag="bank%d" % (n % 4))
             hidden_tile(bank[:], w1_codes, w1_plane, t, x_codes[:, entries], x_plane[:, entries])
             nc.scalar.activation(out=h[t][:, entries], in_=bank[:], func=SILU, bias=zero_bias)
-        first, second = target_halves
-        whole = slice(0, V)
+
+        picked = [[sb([P, 2, V], F32, "picked%d%d" % (d, pair)) for pair in range(2)] for d in range(D)]
+
+        def window(d, t, targets):
+            return h[t][:].indirect(pos_sb[d][:, list_columns(targets)])
+
+        def pick(d, t, targets):
+            nc.scalar.activation(out=picked[d][t // 2][:, t % 2, targets], in_=window(d, t, targets), func=COPY)
+
         for t in range(PACK):
             pick(0, t, whole)
         pick(1, 1, second)
-        for t in range(2, PACK):
-            pick(1, t, whole)
+        pick(1, 2, whole)
+        for targets in (first, second):
+            pick(1, 3, targets)
 
         w3_grouped = [sb([P, 2, P, PACK], BF16, "w3_grouped%d" % pair) for pair in range(2)]
         w3_codes = sb([P, H], U32, "w3_codes")
@@ -174,7 +173,7 @@ def tile_picked_dime_none_e_kernel(tc, xT, aT, w1, w3, w2_words, w2_scales, offs
         nc.vector.tensor_copy(picked[1][0][:, 0, :], window(1, 0, whole))
         nc.vector.tensor_copy(picked[1][0][:, 1, first], window(1, 1, first))
         for pair in range(2):
-            deal_weights(nc.vector.tensor_copy, w3_grouped[pair], w3_raw[1], pair, w3_parts[1], W3_CUT)
+            deal_weights(nc.vector.tensor_copy, w3_grouped[pair], w3_raw[1], pair, w3_parts[1], w3_parts[1].start)
         f_bank = {}
 
         def filters(d, pair):
@@ -197,34 +196,30 @@ def tile_picked_dime_none_e_kernel(tc, xT, aT, w1, w3, w2_words, w2_scales, offs
                 MULT,
             )
 
-        a_grouped.append(sb([P, V, PACK], BF16, "a_grouped1", tag="w3_grouped0"))
-        for targets in target_halves:
-            interleave(nc.vector.tensor_copy, a_grouped[1], a_raw[1], targets)
-        for targets in target_halves:
-            quantize(nc, a_codes[1][:, targets], a_plane[1][:, targets], a_grouped[1][:, targets, :].rearrange("p v j -> p (v j)"))
+        prepare_features(1, "w3_grouped0")
         for pair in range(2):
             filters(1, pair)
         product(0, 0, slice(0, V))
         product(0, 1, slice(0, V))
         product(1, 0, slice(0, V))
-        for targets in target_halves:
+        for targets in (first, second):
             product(1, 1, targets)
 
         z_grouped = sb([P, V, PACK], BF16, "z_grouped")
         z_codes = sb([P, V], U32, "z_codes")
         z_plane = sb([P, V], U8, "z_plane")
-        for u, targets in enumerate(target_halves):
+        for u, targets in enumerate((first, second)):
             nc.vector.tensor_tensor(
                 z_grouped[:, targets, :].rearrange("p (c i) t -> p c t i", i=2),
                 term[0][:, u].rearrange("p t (c i) -> p c t i", i=2),
                 term[1][:, u].rearrange("p t (c i) -> p c t i", i=2),
                 ADD,
             )
-        for targets in target_halves:
+        for targets in (first, second):
             quantize(nc, z_codes[:, targets], z_plane[:, targets], z_grouped[:, targets, :].rearrange("p v t -> p (v t)"))
 
         result = [sb([P, V], F32, "result%d" % b) for b in range(N // P)]
-        for u, targets in enumerate(target_halves):
+        for u, targets in enumerate((first, second)):
             for b, copy in enumerate((nc.scalar.copy, nc.vector.tensor_copy)):
                 bank = psum.tile([P, P], F32, name="out_bank%d%d" % (u, b), tag="bank%d" % (2 * u + b))
                 nc.tensor.matmul_mx(

@@ -64,7 +64,8 @@ def tile_picked_dime_none_e_kernel(tc, xT, aT, w1, w3, w2_words, w2_scales, offs
         w1_raw = [sb([P, PACK, PACK * (ms.stop - ms.start)], F32, "w1_raw%d" % u) for u, ms in enumerate(w1_parts)]
         w3_parts = [slice(0, P // 2), slice(P // 2, P)]
         w3_raw = [sb([P, PACK, H // 2], F32, "w3_raw%d" % u) for u in range(2)]
-        x_raw = [sb([P, T], F32, "x_raw%d" % j) for j in range(PACK)]
+        x_pair = sb([P, 2, T], F32, "x_pair")
+        x_raw = [x_pair[:, 0, :], x_pair[:, 1, :]] + [sb([P, T], F32, "x_raw%d" % j)[:] for j in range(2, PACK)]
         a_raw = [sb([P, PACK, V], F32, "a_raw%d" % d) for d in range(D)]
         w2_codes = sb([P, 2 * N], U8, "w2_codes")
         w2_plane = sb([P, N], U8, "w2_plane")
@@ -79,18 +80,18 @@ def tile_picked_dime_none_e_kernel(tc, xT, aT, w1, w3, w2_words, w2_scales, offs
         a_rows = aT.rearrange("(p j) u -> p j u", j=PACK)
         w3_rows = w3.rearrange("(p j) c -> p j c", j=PACK)
         w1_rows = w1.rearrange("(p j) c -> p j c", j=PACK)
-        nc.sync.dma_start(out=x_raw[0][:], in_=x_rows[:, 0, :])
+        nc.sync.dma_start(out=x_pair[:], in_=x_rows[:, 0:2, :])
         nc.sync.dma_start(offs_sb[:], offs)
-        for j in range(1, PACK):
-            nc.sync.dma_start(out=x_raw[j][:], in_=x_rows[:, j, :])
+        for j in range(2, PACK):
+            nc.sync.dma_start(out=x_raw[j], in_=x_rows[:, j, :])
         for u, ms in enumerate(w1_parts):
             nc.sync.dma_start(out=w1_raw[u][:], in_=w1_rows[:, :, PACK * ms.start:PACK * ms.stop])
-        nc.sync.dma_start(pos_sb[0][:], pos1)
         nc.sync.dma_start(out=a_raw[0][:], in_=a_rows[:, :, :V])
         nc.sync.dma_start(out=w3_raw[0][:], in_=w3_rows[:, :, :H // 2])
-        nc.sync.dma_start(pos_sb[1][:], pos2)
+        nc.sync.dma_start(pos_sb[0][:], pos1)
         nc.sync.dma_start(out=w3_raw[1][:], in_=w3_rows[:, :, H // 2:])
         nc.sync.dma_start(out=a_raw[1][:], in_=a_rows[:, :, V:])
+        nc.sync.dma_start(pos_sb[1][:], pos2)
         nc.sync.dma_start(out=w2_codes[:].bitcast(I32), in_=w2_words[0].bitcast(I32))
         for q in range(P // QUADRANT):
             nc.sync.dma_start(
@@ -101,8 +102,12 @@ def tile_picked_dime_none_e_kernel(tc, xT, aT, w1, w3, w2_words, w2_scales, offs
         halves = [slice(u * S // 2, (u + 1) * S // 2) for u in range(2)]
         x_grouped = [sb([P, S // 2, PACK], BF16, "x_grouped%d" % u) for u in range(2)]
         for j in range(PACK):
-            nc.vector.tensor_copy(x_grouped[0][:, :, j], x_raw[j][:].indirect(offs_sb[:, list_columns(halves[0])]))
-            nc.scalar.activation(out=x_grouped[1][:, :, j], in_=x_raw[j][:].indirect(offs_sb[:, list_columns(halves[1])]), func=COPY)
+            nc.vector.tensor_copy(x_grouped[0][:, :, j], x_raw[j].indirect(offs_sb[:, list_columns(halves[0])]))
+            looked_up = x_raw[j].indirect(offs_sb[:, list_columns(halves[1])])
+            if j < 2:
+                nc.vector.tensor_copy(x_grouped[1][:, :, j], looked_up)
+            else:
+                nc.scalar.activation(out=x_grouped[1][:, :, j], in_=looked_up, func=COPY)
         x_plane = sb([P, S], U8, "x_plane")
         x_codes = sb([P, S], U32, "x_codes")
         for u in range(2):
@@ -148,7 +153,7 @@ def tile_picked_dime_none_e_kernel(tc, xT, aT, w1, w3, w2_words, w2_scales, offs
         for n, (t, entries) in enumerate(pieces):
             bank = psum.tile([P, entries.stop - entries.start], F32, name="h_bank%d" % n, tag="bank%d" % (n % 4))
             hidden_tile(bank[:], w1_codes, w1_plane, t, x_codes[:, entries], x_plane[:, entries])
-            nc.scalar.activation(out=h[t][:, entries], in_=bank[:], func=SILU, bias=zero_bias)
+            nc.scalar.activation(out=h[t][:, entries], in_=bank[:], func=SILU, bias=zero_bias if n == 0 else 0.0)
 
         picked = [[sb([P, 2, V], F32, "picked%d%d" % (d, pair)) for pair in range(2)] for d in range(D)]
 
@@ -158,10 +163,11 @@ def tile_picked_dime_none_e_kernel(tc, xT, aT, w1, w3, w2_words, w2_scales, offs
         def pick(d, t, targets):
             nc.scalar.activation(out=picked[d][t // 2][:, t % 2, targets], in_=window(d, t, targets), func=COPY)
 
-        for t in range(PACK):
+        pick(0, 1, second)
+        for t in range(2, PACK):
             pick(0, t, whole)
-        pick(1, 1, second)
-        pick(1, 2, whole)
+        for t in range(PACK - 1):
+            pick(1, t, whole)
         for targets in (first, second):
             pick(1, 3, targets)
 
@@ -170,8 +176,8 @@ def tile_picked_dime_none_e_kernel(tc, xT, aT, w1, w3, w2_words, w2_scales, offs
         w3_plane = sb([P, H], U8, "w3_plane")
         for pair in range(2):
             deal_weights(nc.vector.tensor_copy, w3_grouped[pair], w3_raw[0], pair, w3_parts[0], 0)
-        nc.vector.tensor_copy(picked[1][0][:, 0, :], window(1, 0, whole))
-        nc.vector.tensor_copy(picked[1][0][:, 1, first], window(1, 1, first))
+        nc.vector.tensor_copy(picked[0][0][:, 0, :], window(0, 0, whole))
+        nc.vector.tensor_copy(picked[0][0][:, 1, first], window(0, 1, first))
         for pair in range(2):
             deal_weights(nc.vector.tensor_copy, w3_grouped[pair], w3_raw[1], pair, w3_parts[1], w3_parts[1].start)
         f_bank = {}

from contextlib import ExitStack

import concourse.mybir as mybir

K, T, S, V, H, N = 512, 2048, 512, 256, 512, 256
D = 2
FLOPS = 2 * K * H * S + 2 * K * H * D * V + 2 * H * N * V

F32 = mybir.dt.float32
BF16 = mybir.dt.bfloat16
I32 = mybir.dt.int32
U32 = mybir.dt.uint32
U16 = mybir.dt.uint16
U8 = mybir.dt.uint8
FP8X4 = mybir.dt.float8_e4m3fn_x4
FP4X4 = mybir.dt.float4_e2m1fn_x4
SILU = mybir.ActivationFunctionType.Silu
COPY = mybir.ActivationFunctionType.Copy
MULT = mybir.AluOpType.mult
ADD = mybir.AluOpType.add

P = 128
PACK = 4
LINE = 4
LIST_COLUMN = 16
QUADRANT = 32
W1_CUTS = (0, 64, 96, 128)


def deal_weights(copy, grouped, raw, pair, ms, first=0):
    copy(
        out=grouped[:].rearrange("p e m j -> p m j e")[:, ms],
        in_=raw[:].rearrange("p j (m t) -> p m j t", t=PACK)[:, ms.start - first:ms.stop - first, :, 2 * pair:2 * pair + 2],
    )


def interleave(copy, grouped, raw, targets):
    copy(
        out=grouped[:, targets, :].rearrange("p (c i) j -> p c j i", i=LINE),
        in_=raw[:, :, targets].rearrange("p j (c i) -> p c j i", i=LINE),
    )


def quantize(nc, codes, plane, grouped):
    nc.vector.quantize_mx(out=codes.bitcast(FP8X4), scales=plane, in_=grouped)


def list_columns(entries):
    return slice(entries.start // LIST_COLUMN, entries.stop // LIST_COLUMN)


def tile_picked_dime_none_e_kernel(tc, xT, aT, w1, w3, w2_words, w2_scales, offs, pos1, pos2, out):
    nc = tc.nc
    with ExitStack() as ctx:
        keep = ctx.enter_context(tc.tile_pool(name="keep", bufs=1))
        psum = ctx.enter_context(tc.psum_pool(name="psum", bufs=1))

        def sb(shape, dtype, name, tag=None):
            return keep.tile(shape, dtype, name=name, tag=tag or name, align_bytes=256)

        offs_sb = sb([P, S // LIST_COLUMN], U16, "offs_sb")
        pos_sb = [sb([P, V // LIST_COLUMN], U16, "pos%d_sb" % d) for d in range(D)]
        w1_parts = [slice(W1_CUTS[u], W1_CUTS[u + 1]) for u in range(3)]
        w1_raw = [sb([P, PACK, PACK * (ms.stop - ms.start)], F32, "w1_raw%d" % u) for u, ms in enumerate(w1_parts)]
        w3_parts = [slice(0, P // 2), slice(P // 2, P)]
        w3_raw = [sb([P, PACK, H // 2], F32, "w3_raw%d" % u) for u in range(2)]
        x_pair = sb([P, 2, T], F32, "x_pair")
        x_raw = [x_pair[:, 0, :], x_pair[:, 1, :]] + [sb([P, T], F32, "x_raw%d" % j)[:] for j in range(2, PACK)]
        a_raw = [sb([P, PACK, V], F32, "a_raw%d" % d) for d in range(D)]
        w2_codes = sb([P, 2 * N], U8, "w2_codes")
        w2_plane = sb([P, N], U8, "w2_plane")
        zeros = sb([P, 2], F32, "zeros")

        nc.vector.memset(zeros[:, 0:1], 0.0)
        nc.vector.memset(w2_plane[:].bitcast(I32), 0)
        zero_bias = zeros[:, 1:2]
        nc.scalar.activation(out=zero_bias, in_=zeros[:, 0:1], func=SILU)

        x_rows = xT.rearrange("(p j) t -> p j t", j=PACK)
        a_rows = aT.rearrange("(p j) u -> p j u", j=PACK)
        w3_rows = w3.rearrange("(p j) c -> p j c", j=PACK)
        w1_rows = w1.rearrange("(p j) c -> p j c", j=PACK)
        nc.sync.dma_start(out=x_pair[:], in_=x_rows[:, 0:2, :])
        nc.sync.dma_start(offs_sb[:], offs)
        for j in range(2, PACK):
            nc.sync.dma_start(out=x_raw[j], in_=x_rows[:, j, :])
        for u, ms in enumerate(w1_parts):
            nc.sync.dma_start(out=w1_raw[u][:], in_=w1_rows[:, :, PACK * ms.start:PACK * ms.stop])
        nc.sync.dma_start(out=a_raw[0][:], in_=a_rows[:, :, :V])
        nc.sync.dma_start(out=w3_raw[0][:], in_=w3_rows[:, :, :H // 2])
        nc.sync.dma_start(pos_sb[0][:], pos1)
        nc.sync.dma_start(out=w3_raw[1][:], in_=w3_rows[:, :, H // 2:])
        nc.sync.dma_start(out=a_raw[1][:], in_=a_rows[:, :, V:])
        nc.sync.dma_start(pos_sb[1][:], pos2)
        nc.sync.dma_start(out=w2_codes[:].bitcast(I32), in_=w2_words[0].bitcast(I32))
        for q in range(P // QUADRANT):
            nc.sync.dma_start(
                out=w2_plane[QUADRANT * q:QUADRANT * q + 4, :].bitcast(I32),
                in_=w2_scales[0, 4 * q:4 * q + 4, :].bitcast(I32),
            )

        halves = [slice(u * S // 2, (u + 1) * S // 2) for u in range(2)]
        x_grouped = [sb([P, S // 2, PACK], BF16, "x_grouped%d" % u) for u in range(2)]
        for j in range(PACK):
            nc.vector.tensor_copy(x_grouped[0][:, :, j], x_raw[j].indirect(offs_sb[:, list_columns(halves[0])]))
            looked_up = x_raw[j].indirect(offs_sb[:, list_columns(halves[1])])
            if j < 2:
                nc.vector.tensor_copy(x_grouped[1][:, :, j], looked_up)
            else:
                nc.scalar.activation(out=x_grouped[1][:, :, j], in_=looked_up, func=COPY)
        x_plane = sb([P, S], U8, "x_plane")
        x_codes = sb([P, S], U32, "x_codes")
        for u in range(2):
            quantize(nc, x_codes[:, halves[u]], x_plane[:, halves[u]], x_grouped[u][:].rearrange("p s j -> p (s j)"))

        w1_grouped = [sb([P, 2, P, PACK], BF16, "w1_grouped%d" % pair) for pair in range(2)]
        w1_codes = sb([P, H], U32, "w1_codes")
        w1_plane = sb([P, H], U8, "w1_plane")
        for u in range(3):
            for pair, copy in enumerate((nc.vector.tensor_copy, nc.scalar.copy if u < 2 else nc.vector.tensor_copy)):
                deal_weights(copy, w1_grouped[pair], w1_raw[u], pair, w1_parts[u], w1_parts[u].start)
        for t0, t1 in ((0, 1), (1, 2), (2, 4)):
            columns = slice(t0 * P, t1 * P)
            quantize(nc, w1_codes[:, columns], w1_plane[:, columns], w1_grouped[t0 // 2][:, t0 % 2:(t1 - 1) % 2 + 1].rearrange("p e m j -> p (e m j)"))

        def hidden_tile(bank, w_codes, w_plane, t, codes, plane):
            nc.tensor.matmul_mx(
                out=bank,
                lhsT=w_codes[:, t * P:(t + 1) * P].bitcast(FP8X4),
                lhsT_scale=w_plane[:, t * P:(t + 1) * P],
                rhs=codes.bitcast(FP8X4),
                rhs_scale=plane,
                start=True,
                stop=True,
            )

        first, second = [slice(u * P, (u + 1) * P) for u in range(V // P)]
        whole = slice(0, V)
        a_codes = [sb([P, V], U32, "a_codes%d" % d) for d in range(D)]
        a_plane = [sb([P, V], U8, "a_plane%d" % d) for d in range(D)]

        def prepare_features(d, tag):
            grouped = sb([P, V, PACK], BF16, "a_grouped%d" % d, tag=tag)
            for targets in (first, second):
                interleave(nc.vector.tensor_copy, grouped, a_raw[d], targets)
            for targets in (first, second):
                quantize(nc, a_codes[d][:, targets], a_plane[d][:, targets], grouped[:, targets, :].rearrange("p v j -> p (v j)"))

        prepare_features(0, "a_grouped0")

        h = [sb([P, S], F32, "h%d" % t) for t in range(PACK)]
        pieces = [(0, slice(0, P)), (0, slice(P, 2 * P)), (0, halves[1])] + [(t, slice(0, S)) for t in range(1, PACK)]
        for n, (t, entries) in enumerate(pieces):
            bank = psum.tile([P, entries.stop - entries.start], F32, name="h_bank%d" % n, tag="bank%d" % (n % 4))
            hidden_tile(bank[:], w1_codes, w1_plane, t, x_codes[:, entries], x_plane[:, entries])
            nc.scalar.activation(out=h[t][:, entries], in_=bank[:], func=SILU, bias=zero_bias if n == 0 else 0.0)

        picked = [[sb([P, 2, V], F32, "picked%d%d" % (d, pair)) for pair in range(2)] for d in range(D)]

        def window(d, t, targets):
            return h[t][:].indirect(pos_sb[d][:, list_columns(targets)])

        def pick(d, t, targets):
            nc.scalar.activation(out=picked[d][t // 2][:, t % 2, targets], in_=window(d, t, targets), func=COPY)

        pick(0, 1, second)
        for t in range(2, PACK):
            pick(0, t, whole)
        for t in range(PACK - 1):
            pick(1, t, whole)
        for targets in (first, second):
            pick(1, 3, targets)

        w3_grouped = [sb([P, 2, P, PACK], BF16, "w3_grouped%d" % pair) for pair in range(2)]
        w3_codes = sb([P, H], U32, "w3_codes")
        w3_plane = sb([P, H], U8, "w3_plane")
        for pair in range(2):
            deal_weights(nc.vector.tensor_copy, w3_grouped[pair], w3_raw[0], pair, w3_parts[0], 0)
        nc.vector.tensor_copy(picked[0][0][:, 0, :], window(0, 0, whole))
        nc.vector.tensor_copy(picked[0][0][:, 1, first], window(0, 1, first))
        for pair in range(2):
            deal_weights(nc.vector.tensor_copy, w3_grouped[pair], w3_raw[1], pair, w3_parts[1], w3_parts[1].start)
        f_bank = {}

        def filters(d, pair):
            f_bank[d, pair] = psum.tile([P, 2, V], F32, name="f_bank%d%d" % (d, pair), tag="bank%d" % (4 + 2 * d + pair))
            for e in range(2):
                hidden_tile(f_bank[d, pair][:, e, :], w3_codes, w3_plane, 2 * pair + e, a_codes[d][:, :], a_plane[d][:, :])

        for pair in range(2):
            columns = slice(2 * pair * P, 2 * (pair + 1) * P)
            quantize(nc, w3_codes[:, columns], w3_plane[:, columns], w3_grouped[pair][:].rearrange("p e m j -> p (e m j)"))
            filters(0, pair)

        term = [sb([P, V // P, PACK, P], F32, "term%d" % d) for d in range(D)]

        def product(d, pair, targets):
            nc.vector.tensor_tensor(
                term[d][:, targets.start // P:targets.stop // P, 2 * pair:2 * pair + 2, :].rearrange("p u e v -> p e u v"),
                f_bank[d, pair][:, :, targets].rearrange("p e (u v) -> p e u v", v=P),
                picked[d][pair][:, :, targets].rearrange("p e (u v) -> p e u v", v=P),
                MULT,
            )

        prepare_features(1, "w3_grouped0")
        for pair in range(2):
            filters(1, pair)
        product(0, 0, slice(0, V))
        product(0, 1, slice(0, V))
        product(1, 0, slice(0, V))
        for targets in (first, second):
            product(1, 1, targets)

        z_grouped = sb([P, V, PACK], BF16, "z_grouped")
        z_codes = sb([P, V], U32, "z_codes")
        z_plane = sb([P, V], U8, "z_plane")
        for u, targets in enumerate((first, second)):
            nc.vector.tensor_tensor(
                z_grouped[:, targets, :].rearrange("p (c i) t -> p c t i", i=2),
                term[0][:, u].rearrange("p t (c i) -> p c t i", i=2),
                term[1][:, u].rearrange("p t (c i) -> p c t i", i=2),
                ADD,
            )
        for targets in (first, second):
            quantize(nc, z_codes[:, targets], z_plane[:, targets], z_grouped[:, targets, :].rearrange("p v t -> p (v t)"))

        result = [sb([P, V], F32, "result%d" % b) for b in range(N // P)]
        for u, targets in enumerate((first, second)):
            for b, copy in enumerate((nc.scalar.copy, nc.vector.tensor_copy)):
                bank = psum.tile([P, P], F32, name="out_bank%d%d" % (u, b), tag="bank%d" % (2 * u + b))
                nc.tensor.matmul_mx(
                    out=bank[:],
                    lhsT=w2_codes[:, 2 * b * P:2 * (b + 1) * P].bitcast(FP4X4),
                    lhsT_scale=w2_plane[:, b * P:(b + 1) * P],
                    rhs=z_codes[:, targets].bitcast(FP8X4),
                    rhs_scale=z_plane[:, targets],
                    start=True,
                    stop=True,
                )
                copy(out=result[b][:, targets], in_=bank[:])
                queue = nc.scalar if (u, b) == (1, 0) else nc.sync
                queue.dma_start(out=out[b * P:(b + 1) * P, targets], in_=result[b][:, targets])
